import numpy as np
import ml_dtypes


def mxq(x, axis, fmt="e4m3"):
    dtype, down = {"e4m3": (ml_dtypes.float8_e4m3fn, 7), "e5m2": (ml_dtypes.float8_e5m2, 14)}[fmt]
    v = np.moveaxis(np.asarray(x, np.float32).astype(ml_dtypes.bfloat16).astype(np.float64), axis, -1)
    blocks = v.reshape(v.shape[:-1] + (-1, 32))
    amax = np.abs(blocks).max(-1, keepdims=True)
    byte = np.maximum(np.where(amax > 0, np.frexp(amax)[1] - 1 + 127, 0) - down, 1)
    scale = np.exp2(byte - 127.0)
    codes = (blocks / scale).astype(np.float32).astype(dtype).astype(np.float64)
    return np.moveaxis((codes * scale).reshape(v.shape), -1, axis)


WIDE = False


def mx_kscale(k):
    if not WIDE:
        return np.ones(k)
    levels = np.array([10, -10, 5, -5, 0])
    if k % 512:
        return np.exp2(np.random.permutation(np.resize(levels, k // 32))).repeat(32)
    a = np.empty((k // 512, 16))
    for p in range(k // 512):
        a[p, :8] = np.random.permutation(np.resize(levels, 8))
        for g in range(8):
            far = levels[np.abs(levels - a[p, g]) >= 10]
            a[p, g + 8] = far[np.random.randint(len(far))]
    return np.exp2(a.ravel()).repeat(32)


def f64(x):
    return np.asarray(x).astype(np.float64)


def striped(idx):
    return np.tile(np.asarray(idx).reshape(-1, 16).T, (8, 1)).astype(np.uint16)


def unstriped(offs):
    return offs[:16].T.reshape(-1).astype(np.int64)


E2M1 = np.array([0.0, 0.5, 1.0, 1.5, 2.0, 3.0, 4.0, 6.0, -0.0, -0.5, -1.0, -1.5, -2.0, -3.0, -4.0, -6.0])


def pack_weight(w, fmt):
    k, n = w.shape
    w = f64(np.asarray(w, np.float32).astype(ml_dtypes.bfloat16)).reshape(k // 32, 32, n)
    amax = np.abs(w).max(1)
    if fmt == "e4m3":
        byte = np.frexp(amax)[1] - 1 + 127 - 7
    else:
        mant, ex = np.frexp(amax / 6.0)
        byte = np.where(mant > 0.5, ex, ex - 1) + 127
    byte = np.clip(np.where(amax > 0, byte, 1), 1, 254)
    scaled = (w * np.exp2(127.0 - byte)[:, None, :]).reshape(k, n).astype(np.float32)
    by_word = np.ascontiguousarray(scaled.reshape(k // 512, 128, 4, n).transpose(0, 1, 3, 2))
    if fmt == "e4m3":
        words = by_word.astype(ml_dtypes.float8_e4m3fn).view(np.uint8)
    else:
        c = by_word.astype(ml_dtypes.float4_e2m1fn).view(np.uint8) & 0xF
        words = (c[..., 0::2] | (c[..., 1::2] << 4)).reshape(k // 512, 128, 2 * n)
    return np.ascontiguousarray(words), np.ascontiguousarray(byte.astype(np.uint8).reshape(k // 512, 16, n))


def unpack_weight(words, scales, fmt):
    g, _, n = scales.shape
    words = np.ascontiguousarray(words).reshape(g, 128, n, -1)
    if fmt == "e4m3":
        vals = words.view(ml_dtypes.float8_e4m3fn).astype(np.float64)
    else:
        nib = np.empty((g, 128, n, 4), np.uint8)
        nib[..., 0::2] = words & 0xF
        nib[..., 1::2] = words >> 4
        vals = E2M1[nib]
    vals = vals * np.repeat(np.exp2(scales.astype(np.float64) - 127.0), 8, axis=1)[..., None]
    return vals.transpose(0, 1, 3, 2).reshape(g * 512, n)


def bf(x):
    return np.asarray(x, np.float32).astype(ml_dtypes.bfloat16)


def planes(Y):
    r, m = Y.shape
    b = f64(bf(Y)).reshape(r // 32, 32, m)
    amax = np.abs(b).max(1)
    byte = np.clip(np.where(amax > 0, np.frexp(amax)[1] - 1 + 127 - 7, 1), 1, 254)
    codes = (b * np.exp2(127.0 - byte)[:, None, :]).reshape(r, m).astype(np.float32).astype(ml_dtypes.float8_e4m3fn).view(np.uint8)
    words = codes.reshape(r // 512, 128, 4, m).transpose(0, 1, 3, 2)
    return np.ascontiguousarray(words), np.ascontiguousarray(byte.astype(np.uint8).reshape(r // 512, 16, m))


B, N, T, D, NQ = 1, 512, 2048, 512, 256


def setup_inputs():
    n = np.random.standard_normal
    idx = np.random.permutation(T)[:B * N]
    s = mx_kscale(D)[:, None]
    kp = pack_weight(n((D, T)) / s, "e4m3")
    cp = pack_weight(n((D, T)) / s, "e4m3")
    return {
        "qT": (n((B, D, NQ)) * s * (1.00 / np.sqrt(D))).astype(np.float32),
        "k_words": kp[0],
        "k_scales": kp[1],
        "c_words": cp[0],
        "c_scales": cp[1],
        "offs": striped(idx),
    }


def reference(qT, k_words, k_scales, c_words, c_scales, offs):
    idx = unstriped(offs)
    pick = lambda x, which: x[:, which].reshape(x.shape[0], B, -1).transpose(1, 0, 2)
    k = unpack_weight(k_words, k_scales, "e4m3")
    kg = pick(k, idx)
    c = unpack_weight(c_words, c_scales, "e4m3")
    cg = pick(c, idx)
    qq = mxq(f64(qT), 1, "e4m3")
    a = kg.transpose(0, 2, 1) @ qq
    z = cg.transpose(0, 2, 1) @ qq
    y = np.maximum(a, 0.0) * z
    Y = y[0]
    words, scales = planes(Y)
    return Y, words, scales

@@ -1,0 +1,120 @@
+from contextlib import ExitStack
+
+import concourse.mybir as mybir
+
+SLOTS, POOL, D, NQ = 512, 2048, 512, 256
+FLOPS = 2 * 2 * SLOTS * D * NQ
+
+F32 = mybir.dt.float32
+BF16 = mybir.dt.bfloat16
+I32 = mybir.dt.int32
+U32 = mybir.dt.uint32
+U16 = mybir.dt.uint16
+U8 = mybir.dt.uint8
+FP8X4 = mybir.dt.float8_e4m3fn_x4
+ALU = mybir.AluOpType
+
+P = 128
+PACK = 4
+HALF = NQ // 2
+GATE_ROW = 4
+
+
+def tile_attend_plh_reglu_topk_kernel(tc, qT, k_words, k_scales, c_words, c_scales, offs, out_0, out_1, out_2):
+    nc = tc.nc
+    with ExitStack() as ctx:
+        sb = ctx.enter_context(tc.tile_pool(name="sb", bufs=1))
+        ps = ctx.enter_context(tc.psum_pool(name="ps", bufs=1))
+
+        offsets = sb.tile([P, SLOTS // 16], U16, name="offsets")
+        c_bytes = sb.tile([P, POOL], U8, name="c_bytes", align_bytes=64)
+        k_bytes = sb.tile([P, POOL], U8, name="k_bytes", align_bytes=64)
+        c_pool = sb.tile([P, POOL], I32, name="c_pool", align_bytes=64)
+        k_pool = sb.tile([P, POOL], I32, name="k_pool", align_bytes=64)
+        q_raw = sb.tile([P, PACK, NQ], F32, name="q_raw", align_bytes=64)
+
+        nc.vector.memset(c_bytes[:].bitcast(I32), 0)
+        nc.gpsimd.memset(k_bytes[:].bitcast(I32), 0)
+        nc.sync.dma_start(offsets[:], offs)
+
+        def load_scale_rows(queue, tile, scales, quadrant, row):
+            first = 32 * quadrant + row
+            queue.dma_start(tile[first : first + 4, :].bitcast(I32), scales[0, 4 * quadrant : 4 * quadrant + 4, :].bitcast(I32))
+
+        def load_words(tile, words):
+            nc.sync.dma_start(tile[:], words[0].rearrange("p t r -> p (t r)").bitcast(I32))
+
+        for quadrant in range(4):
+            load_scale_rows(nc.scalar, c_bytes, c_scales, quadrant, 0)
+        load_words(c_pool, c_words)
+        nc.sync.dma_start(q_raw[:], qT[0].rearrange("(p j) q -> p j q", j=PACK))
+        load_words(k_pool, k_words)
+        for quadrant in range(4):
+            load_scale_rows(nc.scalar if quadrant < 2 else nc.gpsimd, k_bytes, k_scales, quadrant, GATE_ROW)
+
+        def gather_scales(name, window):
+            listed = sb.tile([P, SLOTS], U8, name=name + "_listed", align_bytes=64)
+            dealt = sb.tile([P, SLOTS], U8, name=name + "_dealt", align_bytes=64)
+            nc.vector.tensor_copy(listed[:], window[:].indirect(offsets[:]))
+            nc.vector.tensor_copy(dealt[:].rearrange("p (r s) -> p r s", r=PACK), listed[:].rearrange("p (s r) -> p r s", r=PACK))
+            return dealt
+
+        def gather_words(name, window):
+            dealt = sb.tile([P, SLOTS], U32, name=name, align_bytes=64)
+            nc.vector.tensor_copy(dealt[:].rearrange("p (r s) -> p s r", r=PACK), window[:].bitcast(U32).indirect(offsets[:]))
+            return dealt
+
+        c_sc = gather_scales("c_sc", c_bytes)
+        c_cols = gather_words("c_cols", c_pool)
+
+        q_bf = sb.tile([P, NQ, PACK], BF16, name="q_bf", align_bytes=64)
+        nc.scalar.copy(q_bf[:].rearrange("p (c i) t -> p c t i", i=4), q_raw[:].rearrange("p t (c i) -> p c t i", i=4))
+        q_codes = sb.tile([P, NQ], U32, name="q_codes", align_bytes=64)
+        q_sc = sb.tile([P, NQ], U8, name="q_sc", align_bytes=64)
+        nc.vector.quantize_mx(out=q_codes[:].bitcast(FP8X4), scales=q_sc[:], in_=q_bf[:].rearrange("p q t -> p (q t)"))
+
+        k_sc = gather_scales("k_sc", k_bytes)
+        k_cols = gather_words("k_cols", k_pool)
+
+        z_sb = sb.tile([P, 2, PACK, HALF], F32, name="z_sb", align_bytes=64)
+        for pair in range(2):
+            bank = ps.tile([P, 2, NQ], F32, name=f"z_bank{pair}")
+            for i in range(2):
+                cols = slice((2 * pair + i) * P, (2 * pair + i + 1) * P)
+                nc.tensor.matmul_mx(out=bank[:, i, :], lhsT=c_cols[:, cols].bitcast(FP8X4), lhsT_scale=c_sc[:, cols],
+                                    rhs=q_codes[:].bitcast(FP8X4), rhs_scale=q_sc[:], start=True, stop=True)
+            nc.scalar.copy(z_sb[:, :, 2 * pair : 2 * pair + 2, :], bank[:].rearrange("p i (h q) -> p h i q", h=2))
+
+        y_codes = sb.tile([P, NQ], U32, name="y_codes", align_bytes=64)
+        y_sc = sb.tile([P, NQ], U8, name="y_sc", align_bytes=64)
+        out_rows = out_0.rearrange("(p r) q -> p r q", r=PACK)
+        out_words = out_1[0].rearrange("p q u -> p (q u)").bitcast(I32)
+        y_halves = []
+        for h in range(2):
+            qs = slice(h * HALF, (h + 1) * HALF)
+            y = sb.tile([P, PACK, HALF], F32, name=f"y{h}", align_bytes=64)
+            for pair in range(2):
+                bank = ps.tile([P, 2, HALF], F32, name=f"a_bank{h}{pair}")
+                for i in range(2):
+                    cols = slice((2 * pair + i) * P, (2 * pair + i + 1) * P)
+                    nc.tensor.matmul_mx(out=bank[:, i, :], lhsT=k_cols[:, cols].bitcast(FP8X4), lhsT_scale=k_sc[GATE_ROW:P, cols],
+                                        rhs=q_codes[:, qs].bitcast(FP8X4), rhs_scale=q_sc[:, qs], start=True, stop=True)
+                rs = slice(2 * pair, 2 * pair + 2)
+                nc.vector.scalar_tensor_tensor(out=y[:, rs, :].rearrange("p r q -> p (r q)"), in0=bank[:].rearrange("p r q -> p (r q)"), scalar=0.0,
+                                               in1=z_sb[:, h, rs, :].rearrange("p r q -> p (r q)"), op0=ALU.max, op1=ALU.mult)
+            nc.sync.dma_start(out_rows[:, :, qs], y[:])
+            y_halves.append(y)
+        for h in range(2):
+            qs = slice(h * HALF, (h + 1) * HALF)
+            y_bf = sb.tile([P, HALF, PACK], BF16, name=f"y_bf{h}", align_bytes=64)
+            dst = y_bf[:].rearrange("p (c i) t -> p c t i", i=4)
+            src = y_halves[h][:].rearrange("p t (c i) -> p c t i", i=4)
+            if h == 0:
+                nc.scalar.copy(dst, src)
+            else:
+                nc.vector.tensor_copy(dst, src)
+            nc.vector.quantize_mx(out=y_codes[:, qs].bitcast(FP8X4), scales=y_sc[:, qs], in_=y_bf[:].rearrange("p q t -> p (q t)"))
+        nc.sync.dma_start(out_words, y_codes[:].bitcast(I32))
+        for quadrant in range(4):
+            queue = nc.scalar if quadrant % 2 else nc.sync
+            queue.dma_start(out_2[0, 4 * quadrant : 4 * quadrant + 4, :].bitcast(I32), y_sc[32 * quadrant : 32 * quadrant + 4, :].bitcast(I32))

@@ -18,6 +18,7 @@ P = 128
 PACK = 4
 HALF = NQ // 2
 GATE_ROW = 4
+HEAD = 512
 
 
 def tile_attend_plh_reglu_topk_kernel(tc, qT, k_words, k_scales, c_words, c_scales, offs, out_0, out_1, out_2):
@@ -34,47 +35,53 @@ def tile_attend_plh_reglu_topk_kernel(tc, qT, k_words, k_scales, c_words, c_scal
         q_raw = sb.tile([P, PACK, NQ], F32, name="q_raw", align_bytes=64)
 
         nc.vector.memset(c_bytes[:].bitcast(I32), 0)
-        nc.gpsimd.memset(k_bytes[:].bitcast(I32), 0)
+        nc.vector.memset(k_bytes[:].bitcast(I32), 0)
         nc.sync.dma_start(offsets[:], offs)
 
         def load_scale_rows(queue, tile, scales, quadrant, row):
             first = 32 * quadrant + row
             queue.dma_start(tile[first : first + 4, :].bitcast(I32), scales[0, 4 * quadrant : 4 * quadrant + 4, :].bitcast(I32))
 
-        def load_words(tile, words):
-            nc.sync.dma_start(tile[:], words[0].rearrange("p t r -> p (t r)").bitcast(I32))
+        def load_words(tile, words, first, end):
+            nc.sync.dma_start(tile[:, first:end], words[0].rearrange("p t r -> p (t r)").bitcast(I32)[:, first:end])
 
+        load_words(c_pool, c_words, 0, HEAD)
         for quadrant in range(4):
-            load_scale_rows(nc.scalar, c_bytes, c_scales, quadrant, 0)
-        load_words(c_pool, c_words)
+            load_scale_rows(nc.scalar if quadrant % 2 else nc.sync, c_bytes, c_scales, quadrant, 0)
+        load_words(c_pool, c_words, HEAD, POOL)
         nc.sync.dma_start(q_raw[:], qT[0].rearrange("(p j) q -> p j q", j=PACK))
-        load_words(k_pool, k_words)
         for quadrant in range(4):
-            load_scale_rows(nc.scalar if quadrant < 2 else nc.gpsimd, k_bytes, k_scales, quadrant, GATE_ROW)
+            load_scale_rows(nc.sync, k_bytes, k_scales, quadrant, GATE_ROW)
+        load_words(k_pool, k_words, 0, POOL)
 
-        def gather_scales(name, window):
-            listed = sb.tile([P, SLOTS], U8, name=name + "_listed", align_bytes=64)
-            dealt = sb.tile([P, SLOTS], U8, name=name + "_dealt", align_bytes=64)
+        def gather_scales(name, window, tag):
+            listed = sb.tile([P, SLOTS], U8, name=name, tag=tag, align_bytes=64)
             nc.vector.tensor_copy(listed[:], window[:].indirect(offsets[:]))
+            return listed
+
+        def deal_scales(name, listed):
+            dealt = sb.tile([P, SLOTS], U8, name=name, align_bytes=64)
             nc.vector.tensor_copy(dealt[:].rearrange("p (r s) -> p r s", r=PACK), listed[:].rearrange("p (s r) -> p r s", r=PACK))
             return dealt
 
-        def gather_words(name, window):
-            dealt = sb.tile([P, SLOTS], U32, name=name, align_bytes=64)
+        def gather_words(name, window, tag):
+            dealt = sb.tile([P, SLOTS], U32, name=name, tag=tag, align_bytes=64)
             nc.vector.tensor_copy(dealt[:].rearrange("p (r s) -> p s r", r=PACK), window[:].bitcast(U32).indirect(offsets[:]))
             return dealt
 
-        c_sc = gather_scales("c_sc", c_bytes)
-        c_cols = gather_words("c_cols", c_pool)
+        c_listed = gather_scales("c_listed", c_bytes, "c_listed")
+        c_sc = deal_scales("c_sc", c_listed)
 
+        c_cols = gather_words("c_cols", c_pool, "c_cols")
+        k_listed = gather_scales("k_listed", k_bytes, "k_listed")
         q_bf = sb.tile([P, NQ, PACK], BF16, name="q_bf", align_bytes=64)
         nc.scalar.copy(q_bf[:].rearrange("p (c i) t -> p c t i", i=4), q_raw[:].rearrange("p t (c i) -> p c t i", i=4))
         q_codes = sb.tile([P, NQ], U32, name="q_codes", align_bytes=64)
         q_sc = sb.tile([P, NQ], U8, name="q_sc", align_bytes=64)
         nc.vector.quantize_mx(out=q_codes[:].bitcast(FP8X4), scales=q_sc[:], in_=q_bf[:].rearrange("p q t -> p (q t)"))
 
-        k_sc = gather_scales("k_sc", k_bytes)
-        k_cols = gather_words("k_cols", k_pool)
+        k_sc = deal_scales("k_sc", k_listed)
+        k_cols = gather_words("k_cols", k_pool, "k_cols")
 
         z_sb = sb.tile([P, 2, PACK, HALF], F32, name="z_sb", align_bytes=64)
         for pair in range(2):
@@ -112,9 +119,10 @@ def tile_attend_plh_reglu_topk_kernel(tc, qT, k_words, k_scales, c_words, c_scal
             if h == 0:
                 nc.scalar.copy(dst, src)
             else:
-                nc.vector.tensor_copy(dst, src)
+                nc.scalar.copy(dst[:, :16], src[:, :16])
+                nc.vector.tensor_copy(dst[:, 16:], src[:, 16:])
             nc.vector.quantize_mx(out=y_codes[:, qs].bitcast(FP8X4), scales=y_sc[:, qs], in_=y_bf[:].rearrange("p q t -> p (q t)"))
-        nc.sync.dma_start(out_words, y_codes[:].bitcast(I32))
+            nc.sync.dma_start(out_words[:, qs], y_codes[:, qs].bitcast(I32))
         for quadrant in range(4):
             queue = nc.scalar if quadrant % 2 else nc.sync
             queue.dma_start(out_2[0, 4 * quadrant : 4 * quadrant + 4, :].bitcast(I32), y_sc[32 * quadrant : 32 * quadrant + 4, :].bitcast(I32))

@@ -38,9 +38,8 @@ def tile_attend_plh_reglu_topk_kernel(tc, qT, k_words, k_scales, c_words, c_scal
         nc.vector.memset(k_bytes[:].bitcast(I32), 0)
         nc.sync.dma_start(offsets[:], offs)
 
-        def load_scale_rows(queue, tile, scales, quadrant, row):
-            first = 32 * quadrant + row
-            queue.dma_start(tile[first : first + 4, :].bitcast(I32), scales[0, 4 * quadrant : 4 * quadrant + 4, :].bitcast(I32))
+        def load_scale_rows(queue, tile, scales, f, row):
+            queue.dma_start(tile[:].bitcast(I32)[row + f : P : 32, :], scales[0].bitcast(I32)[f : 16 : 4, :])
 
         def load_words(tile, words, first, end):
             nc.sync.dma_start(tile[:, first:end], words[0].rearrange("p t r -> p (t r)").bitcast(I32)[:, first:end])

@@ -17,7 +17,7 @@ ALU = mybir.AluOpType
 P = 128
 PACK = 4
 HALF = NQ // 2
-GATE_ROW = 4
+ROW_STEP = 8
 HEAD = 512
 
 
@@ -34,62 +34,66 @@ def tile_attend_plh_reglu_topk_kernel(tc, qT, k_words, k_scales, c_words, c_scal
         k_pool = sb.tile([P, POOL], I32, name="k_pool", align_bytes=64)
         q_raw = sb.tile([P, PACK, NQ], F32, name="q_raw", align_bytes=64)
 
-        nc.vector.memset(c_bytes[:].bitcast(I32), 0)
-        nc.vector.memset(k_bytes[:].bitcast(I32), 0)
+        for tile in (c_bytes, k_bytes):
+            nc.vector.memset(tile[:].bitcast(I32)[:, : POOL // 8], 0)
+            nc.gpsimd.memset(tile[:].bitcast(I32)[:, POOL // 8 :], 0)
         nc.sync.dma_start(offsets[:], offs)
 
-        def load_scale_rows(queue, tile, scales, f, row):
-            queue.dma_start(tile[:].bitcast(I32)[row + f : P : 32, :], scales[0].bitcast(I32)[f : 16 : 4, :])
+        def load_scale_rows(tile, scales):
+            nc.sync.dma_start(tile[:].bitcast(I32)[0:P:ROW_STEP, :], scales[0].bitcast(I32))
 
         def load_words(tile, words, first, end):
             nc.sync.dma_start(tile[:, first:end], words[0].rearrange("p t r -> p (t r)").bitcast(I32)[:, first:end])
 
         load_words(c_pool, c_words, 0, HEAD)
-        for quadrant in range(4):
-            load_scale_rows(nc.scalar if quadrant % 2 else nc.sync, c_bytes, c_scales, quadrant, 0)
+        load_scale_rows(c_bytes, c_scales)
+        load_scale_rows(k_bytes, k_scales)
         load_words(c_pool, c_words, HEAD, POOL)
         nc.sync.dma_start(q_raw[:], qT[0].rearrange("(p j) q -> p j q", j=PACK))
-        for quadrant in range(4):
-            load_scale_rows(nc.sync, k_bytes, k_scales, quadrant, GATE_ROW)
         load_words(k_pool, k_words, 0, POOL)
 
-        def gather_scales(name, window, tag):
-            listed = sb.tile([P, SLOTS], U8, name=name, tag=tag, align_bytes=64)
+        def gather_scales(name, window):
+            listed = sb.tile([P, SLOTS], U8, name=name, align_bytes=64)
             nc.vector.tensor_copy(listed[:], window[:].indirect(offsets[:]))
             return listed
 
-        def deal_scales(name, listed):
-            dealt = sb.tile([P, SLOTS], U8, name=name, align_bytes=64)
-            nc.vector.tensor_copy(dealt[:].rearrange("p (r s) -> p r s", r=PACK), listed[:].rearrange("p (s r) -> p r s", r=PACK))
-            return dealt
+        def deal_scales(dealt, listed):
+            nc.vector.tensor_copy(dealt.rearrange("p (r s) -> p r s", r=PACK), listed[:].rearrange("p (s r) -> p r s", r=PACK))
 
         def gather_words(name, window, tag):
             dealt = sb.tile([P, SLOTS], U32, name=name, tag=tag, align_bytes=64)
             nc.vector.tensor_copy(dealt[:].rearrange("p (r s) -> p s r", r=PACK), window[:].bitcast(U32).indirect(offsets[:]))
             return dealt
 
-        c_listed = gather_scales("c_listed", c_bytes, "c_listed")
-        c_sc = deal_scales("c_sc", c_listed)
+        def scale_plane(name, window):
+            listed = gather_scales(name + "_listed", window)
+            plane = sb.tile([P, SLOTS], U8, name=name + "_plane", align_bytes=64)
+            deal_scales(plane[:], listed)
+            for i in range(1, 4):
+                nc.sync.dma_start(plane[:].bitcast(I32)[i:P:32, :], plane[:].bitcast(I32)[ROW_STEP * i : P : 32, :])
+            return plane
+
+        c_sc = scale_plane("c", c_bytes)
+        k_sc = scale_plane("k", k_bytes)
 
         c_cols = gather_words("c_cols", c_pool, "c_cols")
-        k_listed = gather_scales("k_listed", k_bytes, "k_listed")
-        q_bf = sb.tile([P, NQ, PACK], BF16, name="q_bf", align_bytes=64)
+        q_bf = sb.tile([P, NQ, PACK], BF16, name="q_bf", tag="q_bf", align_bytes=64)
         nc.scalar.copy(q_bf[:].rearrange("p (c i) t -> p c t i", i=4), q_raw[:].rearrange("p t (c i) -> p c t i", i=4))
         q_codes = sb.tile([P, NQ], U32, name="q_codes", align_bytes=64)
         q_sc = sb.tile([P, NQ], U8, name="q_sc", align_bytes=64)
         nc.vector.quantize_mx(out=q_codes[:].bitcast(FP8X4), scales=q_sc[:], in_=q_bf[:].rearrange("p q t -> p (q t)"))
 
-        k_sc = deal_scales("k_sc", k_listed)
-        k_cols = gather_words("k_cols", k_pool, "k_cols")
+        k_cols = gather_words("k_cols", k_pool, "q_bf")
 
         z_sb = sb.tile([P, 2, PACK, HALF], F32, name="z_sb", align_bytes=64)
-        for pair in range(2):
-            bank = ps.tile([P, 2, NQ], F32, name=f"z_bank{pair}")
-            for i in range(2):
-                cols = slice((2 * pair + i) * P, (2 * pair + i + 1) * P)
-                nc.tensor.matmul_mx(out=bank[:, i, :], lhsT=c_cols[:, cols].bitcast(FP8X4), lhsT_scale=c_sc[:, cols],
-                                    rhs=q_codes[:].bitcast(FP8X4), rhs_scale=q_sc[:], start=True, stop=True)
-            nc.scalar.copy(z_sb[:, :, 2 * pair : 2 * pair + 2, :], bank[:].rearrange("p i (h q) -> p h i q", h=2))
+        for h in range(2):
+            qs = slice(h * HALF, (h + 1) * HALF)
+            bank = ps.tile([P, PACK, HALF], F32, name=f"z_bank{h}")
+            for r in range(PACK):
+                cols = slice(r * P, (r + 1) * P)
+                nc.tensor.matmul_mx(out=bank[:, r, :], lhsT=c_cols[:, cols].bitcast(FP8X4), lhsT_scale=c_sc[:, cols],
+                                    rhs=q_codes[:, qs].bitcast(FP8X4), rhs_scale=q_sc[:, qs], start=True, stop=True)
+            nc.scalar.copy(z_sb[:, h, :, :], bank[:])
 
         y_codes = sb.tile([P, NQ], U32, name="y_codes", align_bytes=64)
         y_sc = sb.tile([P, NQ], U8, name="y_sc", align_bytes=64)
@@ -103,7 +107,7 @@ def tile_attend_plh_reglu_topk_kernel(tc, qT, k_words, k_scales, c_words, c_scal
                 bank = ps.tile([P, 2, HALF], F32, name=f"a_bank{h}{pair}")
                 for i in range(2):
                     cols = slice((2 * pair + i) * P, (2 * pair + i + 1) * P)
-                    nc.tensor.matmul_mx(out=bank[:, i, :], lhsT=k_cols[:, cols].bitcast(FP8X4), lhsT_scale=k_sc[GATE_ROW:P, cols],
+                    nc.tensor.matmul_mx(out=bank[:, i, :], lhsT=k_cols[:, cols].bitcast(FP8X4), lhsT_scale=k_sc[:, cols],
                                         rhs=q_codes[:, qs].bitcast(FP8X4), rhs_scale=q_sc[:, qs], start=True, stop=True)
                 rs = slice(2 * pair, 2 * pair + 2)
                 nc.vector.scalar_tensor_tensor(out=y[:, rs, :].rearrange("p r q -> p (r q)"), in0=bank[:].rearrange("p r q -> p (r q)"), scalar=0.0,

@@ -35,8 +35,7 @@ def tile_attend_plh_reglu_topk_kernel(tc, qT, k_words, k_scales, c_words, c_scal
         q_raw = sb.tile([P, PACK, NQ], F32, name="q_raw", align_bytes=64)
 
         for tile in (c_bytes, k_bytes):
-            nc.vector.memset(tile[:].bitcast(I32)[:, : POOL // 8], 0)
-            nc.gpsimd.memset(tile[:].bitcast(I32)[:, POOL // 8 :], 0)
+            nc.vector.memset(tile[:].bitcast(I32), 0)
         nc.sync.dma_start(offsets[:], offs)
 
         def load_scale_rows(tile, scales):
@@ -48,8 +47,8 @@ def tile_attend_plh_reglu_topk_kernel(tc, qT, k_words, k_scales, c_words, c_scal
         load_words(c_pool, c_words, 0, HEAD)
         load_scale_rows(c_bytes, c_scales)
         load_scale_rows(k_bytes, k_scales)
-        load_words(c_pool, c_words, HEAD, POOL)
         nc.sync.dma_start(q_raw[:], qT[0].rearrange("(p j) q -> p j q", j=PACK))
+        load_words(c_pool, c_words, HEAD, POOL)
         load_words(k_pool, k_words, 0, POOL)
 
         def gather_scales(name, window):
@@ -65,25 +64,26 @@ def tile_attend_plh_reglu_topk_kernel(tc, qT, k_words, k_scales, c_words, c_scal
             nc.vector.tensor_copy(dealt[:].rearrange("p (r s) -> p s r", r=PACK), window[:].bitcast(U32).indirect(offsets[:]))
             return dealt
 
-        def scale_plane(name, window):
-            listed = gather_scales(name + "_listed", window)
+        def scale_plane(name, listed):
             plane = sb.tile([P, SLOTS], U8, name=name + "_plane", align_bytes=64)
             deal_scales(plane[:], listed)
             for i in range(1, 4):
                 nc.sync.dma_start(plane[:].bitcast(I32)[i:P:32, :], plane[:].bitcast(I32)[ROW_STEP * i : P : 32, :])
             return plane
 
-        c_sc = scale_plane("c", c_bytes)
-        k_sc = scale_plane("k", k_bytes)
+        c_listed = gather_scales("c_listed", c_bytes)
+        k_listed = gather_scales("k_listed", k_bytes)
+        c_sc = scale_plane("c", c_listed)
+        k_sc = scale_plane("k", k_listed)
 
-        c_cols = gather_words("c_cols", c_pool, "c_cols")
         q_bf = sb.tile([P, NQ, PACK], BF16, name="q_bf", tag="q_bf", align_bytes=64)
         nc.scalar.copy(q_bf[:].rearrange("p (c i) t -> p c t i", i=4), q_raw[:].rearrange("p t (c i) -> p c t i", i=4))
         q_codes = sb.tile([P, NQ], U32, name="q_codes", align_bytes=64)
         q_sc = sb.tile([P, NQ], U8, name="q_sc", align_bytes=64)
         nc.vector.quantize_mx(out=q_codes[:].bitcast(FP8X4), scales=q_sc[:], in_=q_bf[:].rearrange("p q t -> p (q t)"))
 
-        k_cols = gather_words("k_cols", k_pool, "q_bf")
+        c_cols = gather_words("c_cols", c_pool, "q_bf")
+        k_cols = gather_words("k_cols", k_pool, "k_cols")
 
         z_sb = sb.tile([P, 2, PACK, HALF], F32, name="z_sb", align_bytes=64)
         for h in range(2):
@@ -99,10 +99,9 @@ def tile_attend_plh_reglu_topk_kernel(tc, qT, k_words, k_scales, c_words, c_scal
         y_sc = sb.tile([P, NQ], U8, name="y_sc", align_bytes=64)
         out_rows = out_0.rearrange("(p r) q -> p r q", r=PACK)
         out_words = out_1[0].rearrange("p q u -> p (q u)").bitcast(I32)
-        y_halves = []
+        y = sb.tile([P, PACK, NQ], F32, name="y", align_bytes=64)
         for h in range(2):
             qs = slice(h * HALF, (h + 1) * HALF)
-            y = sb.tile([P, PACK, HALF], F32, name=f"y{h}", align_bytes=64)
             for pair in range(2):
                 bank = ps.tile([P, 2, HALF], F32, name=f"a_bank{h}{pair}")
                 for i in range(2):
@@ -110,15 +109,14 @@ def tile_attend_plh_reglu_topk_kernel(tc, qT, k_words, k_scales, c_words, c_scal
                     nc.tensor.matmul_mx(out=bank[:, i, :], lhsT=k_cols[:, cols].bitcast(FP8X4), lhsT_scale=k_sc[:, cols],
                                         rhs=q_codes[:, qs].bitcast(FP8X4), rhs_scale=q_sc[:, qs], start=True, stop=True)
                 rs = slice(2 * pair, 2 * pair + 2)
-                nc.vector.scalar_tensor_tensor(out=y[:, rs, :].rearrange("p r q -> p (r q)"), in0=bank[:].rearrange("p r q -> p (r q)"), scalar=0.0,
-                                               in1=z_sb[:, h, rs, :].rearrange("p r q -> p (r q)"), op0=ALU.max, op1=ALU.mult)
-            nc.sync.dma_start(out_rows[:, :, qs], y[:])
-            y_halves.append(y)
+                nc.vector.scalar_tensor_tensor(out=y[:, rs, qs], in0=bank[:], scalar=0.0, in1=z_sb[:, h, rs, :], op0=ALU.max, op1=ALU.mult)
+                if h == 1:
+                    nc.sync.dma_start(out_rows[:, rs, :], y[:, rs, :])
         for h in range(2):
             qs = slice(h * HALF, (h + 1) * HALF)
             y_bf = sb.tile([P, HALF, PACK], BF16, name=f"y_bf{h}", align_bytes=64)
             dst = y_bf[:].rearrange("p (c i) t -> p c t i", i=4)
-            src = y_halves[h][:].rearrange("p t (c i) -> p c t i", i=4)
+            src = y[:, :, qs].rearrange("p t (c i) -> p c t i", i=4)
             if h == 0:
                 nc.scalar.copy(dst, src)
             else:

@@ -31,11 +31,11 @@ def tile_attend_plh_reglu_topk_kernel(tc, qT, k_words, k_scales, c_words, c_scal
         c_bytes = sb.tile([P, POOL], U8, name="c_bytes", align_bytes=64)
         k_bytes = sb.tile([P, POOL], U8, name="k_bytes", align_bytes=64)
         c_pool = sb.tile([P, POOL], I32, name="c_pool", align_bytes=64)
-        k_pool = sb.tile([P, POOL], I32, name="k_pool", align_bytes=64)
+        k_pool = sb.tile([P, POOL], I32, name="k_pool", tag="k_pool", align_bytes=64)
         q_raw = sb.tile([P, PACK, NQ], F32, name="q_raw", align_bytes=64)
 
-        for tile in (c_bytes, k_bytes):
-            nc.vector.memset(tile[:].bitcast(I32), 0)
+        nc.vector.memset(c_bytes[:].bitcast(I32), 0)
+        nc.gpsimd.memset(k_bytes[:].bitcast(I32), 0)
         nc.sync.dma_start(offsets[:], offs)
 
         def load_scale_rows(tile, scales):
@@ -46,7 +46,9 @@ def tile_attend_plh_reglu_topk_kernel(tc, qT, k_words, k_scales, c_words, c_scal
 
         load_words(c_pool, c_words, 0, HEAD)
         load_scale_rows(c_bytes, c_scales)
-        load_scale_rows(k_bytes, k_scales)
+        for i in range(4):
+            queue = nc.scalar if i % 2 else nc.sync
+            queue.dma_start(k_bytes[:].bitcast(I32)[i:P:32, :], k_scales[0].bitcast(I32)[i:16:4, :])
         nc.sync.dma_start(q_raw[:], qT[0].rearrange("(p j) q -> p j q", j=PACK))
         load_words(c_pool, c_words, HEAD, POOL)
         load_words(k_pool, k_words, 0, POOL)
@@ -74,7 +76,13 @@ def tile_attend_plh_reglu_topk_kernel(tc, qT, k_words, k_scales, c_words, c_scal
         c_listed = gather_scales("c_listed", c_bytes)
         k_listed = gather_scales("k_listed", k_bytes)
         c_sc = scale_plane("c", c_listed)
-        k_sc = scale_plane("k", k_listed)
+
+        def gate_plane(pair, tag):
+            plane = sb.tile([P, 2, P], U8, name=f"k_plane{pair}", tag=tag, align_bytes=64)
+            nc.vector.tensor_copy(plane[:], k_listed[:].rearrange("p (s r) -> p r s", r=PACK)[:, 2 * pair : 2 * pair + 2, :])
+            return plane
+
+        k_planes = [gate_plane(0, "k_plane0")]
 
         q_bf = sb.tile([P, NQ, PACK], BF16, name="q_bf", tag="q_bf", align_bytes=64)
         nc.scalar.copy(q_bf[:].rearrange("p (c i) t -> p c t i", i=4), q_raw[:].rearrange("p t (c i) -> p c t i", i=4))
@@ -82,18 +90,20 @@ def tile_attend_plh_reglu_topk_kernel(tc, qT, k_words, k_scales, c_words, c_scal
         q_sc = sb.tile([P, NQ], U8, name="q_sc", align_bytes=64)
         nc.vector.quantize_mx(out=q_codes[:].bitcast(FP8X4), scales=q_sc[:], in_=q_bf[:].rearrange("p q t -> p (q t)"))
 
-        c_cols = gather_words("c_cols", c_pool, "q_bf")
+        c_cols = gather_words("c_cols", c_pool, "c_cols")
         k_cols = gather_words("k_cols", k_pool, "k_cols")
+        k_planes.append(gate_plane(1, "k_pool"))
 
         z_sb = sb.tile([P, 2, PACK, HALF], F32, name="z_sb", align_bytes=64)
         for h in range(2):
             qs = slice(h * HALF, (h + 1) * HALF)
-            bank = ps.tile([P, PACK, HALF], F32, name=f"z_bank{h}")
-            for r in range(PACK):
-                cols = slice(r * P, (r + 1) * P)
-                nc.tensor.matmul_mx(out=bank[:, r, :], lhsT=c_cols[:, cols].bitcast(FP8X4), lhsT_scale=c_sc[:, cols],
-                                    rhs=q_codes[:, qs].bitcast(FP8X4), rhs_scale=q_sc[:, qs], start=True, stop=True)
-            nc.scalar.copy(z_sb[:, h, :, :], bank[:])
+            for pair in range(2):
+                bank = ps.tile([P, 2, HALF], F32, name=f"z_bank{h}{pair}", tag=f"bank{h}{pair}")
+                for i in range(2):
+                    cols = slice((2 * pair + i) * P, (2 * pair + i + 1) * P)
+                    nc.tensor.matmul_mx(out=bank[:, i, :], lhsT=c_cols[:, cols].bitcast(FP8X4), lhsT_scale=c_sc[:, cols],
+                                        rhs=q_codes[:, qs].bitcast(FP8X4), rhs_scale=q_sc[:, qs], start=True, stop=True)
+                nc.scalar.copy(z_sb[:, h, 2 * pair : 2 * pair + 2, :], bank[:])
 
         y_codes = sb.tile([P, NQ], U32, name="y_codes", align_bytes=64)
         y_sc = sb.tile([P, NQ], U8, name="y_sc", align_bytes=64)
@@ -103,10 +113,10 @@ def tile_attend_plh_reglu_topk_kernel(tc, qT, k_words, k_scales, c_words, c_scal
         for h in range(2):
             qs = slice(h * HALF, (h + 1) * HALF)
             for pair in range(2):
-                bank = ps.tile([P, 2, HALF], F32, name=f"a_bank{h}{pair}")
+                bank = ps.tile([P, 2, HALF], F32, name=f"a_bank{h}{pair}", tag=f"bank{h}{pair}")
                 for i in range(2):
                     cols = slice((2 * pair + i) * P, (2 * pair + i + 1) * P)
-                    nc.tensor.matmul_mx(out=bank[:, i, :], lhsT=k_cols[:, cols].bitcast(FP8X4), lhsT_scale=k_sc[:, cols],
+                    nc.tensor.matmul_mx(out=bank[:, i, :], lhsT=k_cols[:, cols].bitcast(FP8X4), lhsT_scale=k_planes[pair][:, i, :],
                                         rhs=q_codes[:, qs].bitcast(FP8X4), rhs_scale=q_sc[:, qs], start=True, stop=True)
                 rs = slice(2 * pair, 2 * pair + 2)
                 nc.vector.scalar_tensor_tensor(out=y[:, rs, qs], in0=bank[:], scalar=0.0, in1=z_sb[:, h, rs, :], op0=ALU.max, op1=ALU.mult)

@@ -17,8 +17,9 @@ ALU = mybir.AluOpType
 P = 128
 PACK = 4
 HALF = NQ // 2
-ROW_STEP = 8
-HEAD = 512
+ROWS = 16
+FIRST_ROW = P - ROWS
+ROW_STEP = P // ROWS
 
 
 def tile_attend_plh_reglu_topk_kernel(tc, qT, k_words, k_scales, c_words, c_scales, offs, out_0, out_1, out_2):
@@ -31,27 +32,22 @@ def tile_attend_plh_reglu_topk_kernel(tc, qT, k_words, k_scales, c_words, c_scal
         c_bytes = sb.tile([P, POOL], U8, name="c_bytes", align_bytes=64)
         k_bytes = sb.tile([P, POOL], U8, name="k_bytes", align_bytes=64)
         c_pool = sb.tile([P, POOL], I32, name="c_pool", align_bytes=64)
-        k_pool = sb.tile([P, POOL], I32, name="k_pool", tag="k_pool", align_bytes=64)
+        k_pool = sb.tile([P, POOL], I32, name="k_pool", align_bytes=64)
         q_raw = sb.tile([P, PACK, NQ], F32, name="q_raw", align_bytes=64)
 
-        nc.vector.memset(c_bytes[:].bitcast(I32), 0)
+        nc.vector.memset(c_bytes[:].bitcast(I32)[:96, :], 0)
+        nc.vector.memset(c_bytes[:].bitcast(I32)[96:FIRST_ROW, :], 0)
         nc.gpsimd.memset(k_bytes[:].bitcast(I32), 0)
         nc.sync.dma_start(offsets[:], offs)
 
-        def load_scale_rows(tile, scales):
-            nc.sync.dma_start(tile[:].bitcast(I32)[0:P:ROW_STEP, :], scales[0].bitcast(I32))
+        def load_words(tile, words):
+            nc.sync.dma_start(tile[:], words[0].rearrange("p t r -> p (t r)").bitcast(I32))
 
-        def load_words(tile, words, first, end):
-            nc.sync.dma_start(tile[:, first:end], words[0].rearrange("p t r -> p (t r)").bitcast(I32)[:, first:end])
-
-        load_words(c_pool, c_words, 0, HEAD)
-        load_scale_rows(c_bytes, c_scales)
-        for i in range(4):
-            queue = nc.scalar if i % 2 else nc.sync
-            queue.dma_start(k_bytes[:].bitcast(I32)[i:P:32, :], k_scales[0].bitcast(I32)[i:16:4, :])
+        nc.sync.dma_start(c_bytes[:].bitcast(I32)[FIRST_ROW:, :], c_scales[0].bitcast(I32))
         nc.sync.dma_start(q_raw[:], qT[0].rearrange("(p j) q -> p j q", j=PACK))
-        load_words(c_pool, c_words, HEAD, POOL)
-        load_words(k_pool, k_words, 0, POOL)
+        nc.sync.dma_start(k_bytes[:].bitcast(I32)[0:P:ROW_STEP, :], k_scales[0].bitcast(I32))
+        load_words(c_pool, c_words)
+        load_words(k_pool, k_words)
 
         def gather_scales(name, window):
             listed = sb.tile([P, SLOTS], U8, name=name, align_bytes=64)
@@ -69,20 +65,16 @@ def tile_attend_plh_reglu_topk_kernel(tc, qT, k_words, k_scales, c_words, c_scal
         def scale_plane(name, listed):
             plane = sb.tile([P, SLOTS], U8, name=name + "_plane", align_bytes=64)
             deal_scales(plane[:], listed)
-            for i in range(1, 4):
-                nc.sync.dma_start(plane[:].bitcast(I32)[i:P:32, :], plane[:].bitcast(I32)[ROW_STEP * i : P : 32, :])
             return plane
 
         c_listed = gather_scales("c_listed", c_bytes)
         k_listed = gather_scales("k_listed", k_bytes)
         c_sc = scale_plane("c", c_listed)
-
-        def gate_plane(pair, tag):
-            plane = sb.tile([P, 2, P], U8, name=f"k_plane{pair}", tag=tag, align_bytes=64)
-            nc.vector.tensor_copy(plane[:], k_listed[:].rearrange("p (s r) -> p r s", r=PACK)[:, 2 * pair : 2 * pair + 2, :])
-            return plane
-
-        k_planes = [gate_plane(0, "k_plane0")]
+        for i in range(4):
+            nc.sync.dma_start(c_sc[:].bitcast(I32)[i:P:32, :], c_sc[:].bitcast(I32)[FIRST_ROW + i : P : 4, :])
+        k_sc = scale_plane("k", k_listed)
+        for i in range(1, 4):
+            nc.sync.dma_start(k_sc[:].bitcast(I32)[i:P:32, :], k_sc[:].bitcast(I32)[ROW_STEP * i : P : 32, :])
 
         q_bf = sb.tile([P, NQ, PACK], BF16, name="q_bf", tag="q_bf", align_bytes=64)
         nc.scalar.copy(q_bf[:].rearrange("p (c i) t -> p c t i", i=4), q_raw[:].rearrange("p t (c i) -> p c t i", i=4))
@@ -92,7 +84,6 @@ def tile_attend_plh_reglu_topk_kernel(tc, qT, k_words, k_scales, c_words, c_scal
 
         c_cols = gather_words("c_cols", c_pool, "c_cols")
         k_cols = gather_words("k_cols", k_pool, "k_cols")
-        k_planes.append(gate_plane(1, "k_pool"))
 
         z_sb = sb.tile([P, 2, PACK, HALF], F32, name="z_sb", align_bytes=64)
         for h in range(2):
@@ -116,7 +107,7 @@ def tile_attend_plh_reglu_topk_kernel(tc, qT, k_words, k_scales, c_words, c_scal
                 bank = ps.tile([P, 2, HALF], F32, name=f"a_bank{h}{pair}", tag=f"bank{h}{pair}")
                 for i in range(2):
                     cols = slice((2 * pair + i) * P, (2 * pair + i + 1) * P)
-                    nc.tensor.matmul_mx(out=bank[:, i, :], lhsT=k_cols[:, cols].bitcast(FP8X4), lhsT_scale=k_planes[pair][:, i, :],
+                    nc.tensor.matmul_mx(out=bank[:, i, :], lhsT=k_cols[:, cols].bitcast(FP8X4), lhsT_scale=k_sc[:, cols],
                                         rhs=q_codes[:, qs].bitcast(FP8X4), rhs_scale=q_sc[:, qs], start=True, stop=True)
                 rs = slice(2 * pair, 2 * pair + 2)
                 nc.vector.scalar_tensor_tensor(out=y[:, rs, qs], in0=bank[:], scalar=0.0, in1=z_sb[:, h, rs, :], op0=ALU.max, op1=ALU.mult)

@@ -26,6 +26,7 @@ def tile_attend_plh_reglu_topk_kernel(tc, qT, k_words, k_scales, c_words, c_scal
     nc = tc.nc
     with ExitStack() as ctx:
         sb = ctx.enter_context(tc.tile_pool(name="sb", bufs=1))
+        reused = ctx.enter_context(tc.tile_pool(name="reused", bufs=1))
         ps = ctx.enter_context(tc.psum_pool(name="ps", bufs=1))
 
         offsets = sb.tile([P, SLOTS // 16], U16, name="offsets")
@@ -33,7 +34,7 @@ def tile_attend_plh_reglu_topk_kernel(tc, qT, k_words, k_scales, c_words, c_scal
         k_bytes = sb.tile([P, POOL], U8, name="k_bytes", align_bytes=64)
         c_pool = sb.tile([P, POOL], I32, name="c_pool", align_bytes=64)
         k_pool = sb.tile([P, POOL], I32, name="k_pool", align_bytes=64)
-        q_raw = sb.tile([P, PACK, NQ], F32, name="q_raw", align_bytes=64)
+        q_raw = reused.tile([P, PACK, NQ], F32, name="q_raw", offset=0, align_bytes=64)
 
         nc.vector.memset(c_bytes[:].bitcast(I32)[:96, :], 0)
         nc.vector.memset(c_bytes[:].bitcast(I32)[96:FIRST_ROW, :], 0)
@@ -62,22 +63,21 @@ def tile_attend_plh_reglu_topk_kernel(tc, qT, k_words, k_scales, c_words, c_scal
             nc.vector.tensor_copy(dealt[:].rearrange("p (r s) -> p s r", r=PACK), window[:].bitcast(U32).indirect(offsets[:]))
             return dealt
 
-        def scale_plane(name, listed):
-            plane = sb.tile([P, SLOTS], U8, name=name + "_plane", align_bytes=64)
-            deal_scales(plane[:], listed)
-            return plane
-
         c_listed = gather_scales("c_listed", c_bytes)
         k_listed = gather_scales("k_listed", k_bytes)
-        c_sc = scale_plane("c", c_listed)
-        for i in range(4):
-            nc.sync.dma_start(c_sc[:].bitcast(I32)[i:P:32, :], c_sc[:].bitcast(I32)[FIRST_ROW + i : P : 4, :])
-        k_sc = scale_plane("k", k_listed)
-        for i in range(1, 4):
-            nc.sync.dma_start(k_sc[:].bitcast(I32)[i:P:32, :], k_sc[:].bitcast(I32)[ROW_STEP * i : P : 32, :])
 
         q_bf = sb.tile([P, NQ, PACK], BF16, name="q_bf", tag="q_bf", align_bytes=64)
         nc.scalar.copy(q_bf[:].rearrange("p (c i) t -> p c t i", i=4), q_raw[:].rearrange("p t (c i) -> p c t i", i=4))
+        c_plane = reused.tile([P, SLOTS], U8, name="c_plane", offset=0, align_bytes=64)
+        k_plane = reused.tile([P, SLOTS], U8, name="k_plane", offset=SLOTS, align_bytes=64)
+        c_sc = c_plane[:]
+        k_sc = k_plane[:]
+        deal_scales(c_sc, c_listed)
+        for i in range(4):
+            nc.sync.dma_start(c_sc.bitcast(I32)[i:P:32, :], c_sc.bitcast(I32)[FIRST_ROW + i : P : 4, :])
+        deal_scales(k_sc, k_listed)
+        for i in range(1, 4):
+            nc.sync.dma_start(k_sc.bitcast(I32)[i:P:32, :], k_sc.bitcast(I32)[ROW_STEP * i : P : 32, :])
         q_codes = sb.tile([P, NQ], U32, name="q_codes", align_bytes=64)
         q_sc = sb.tile([P, NQ], U8, name="q_sc", align_bytes=64)
         nc.vector.quantize_mx(out=q_codes[:].bitcast(FP8X4), scales=q_sc[:], in_=q_bf[:].rearrange("p q t -> p (q t)"))

@@ -36,15 +36,15 @@ def tile_attend_plh_reglu_topk_kernel(tc, qT, k_words, k_scales, c_words, c_scal
         k_pool = sb.tile([P, POOL], I32, name="k_pool", align_bytes=64)
         q_raw = reused.tile([P, PACK, NQ], F32, name="q_raw", offset=0, align_bytes=64)
 
+        nc.vector.memset(k_bytes[:].bitcast(I32), 0)
         nc.vector.memset(c_bytes[:].bitcast(I32)[:96, :], 0)
         nc.vector.memset(c_bytes[:].bitcast(I32)[96:FIRST_ROW, :], 0)
-        nc.gpsimd.memset(k_bytes[:].bitcast(I32), 0)
         nc.sync.dma_start(offsets[:], offs)
 
         def load_words(tile, words):
             nc.sync.dma_start(tile[:], words[0].rearrange("p t r -> p (t r)").bitcast(I32))
 
-        nc.sync.dma_start(c_bytes[:].bitcast(I32)[FIRST_ROW:, :], c_scales[0].bitcast(I32))
+        nc.scalar.dma_start(c_bytes[:].bitcast(I32)[FIRST_ROW:, :], c_scales[0].bitcast(I32))
         nc.sync.dma_start(q_raw[:], qT[0].rearrange("(p j) q -> p j q", j=PACK))
         nc.sync.dma_start(k_bytes[:].bitcast(I32)[0:P:ROW_STEP, :], k_scales[0].bitcast(I32))
         load_words(c_pool, c_words)

@@ -18,7 +18,7 @@ P = 128
 PACK = 4
 HALF = NQ // 2
 ROWS = 16
-FIRST_ROW = P - ROWS
+C_ROW = P - ROWS
 ROW_STEP = P // ROWS
 
 
@@ -26,7 +26,6 @@ def tile_attend_plh_reglu_topk_kernel(tc, qT, k_words, k_scales, c_words, c_scal
     nc = tc.nc
     with ExitStack() as ctx:
         sb = ctx.enter_context(tc.tile_pool(name="sb", bufs=1))
-        reused = ctx.enter_context(tc.tile_pool(name="reused", bufs=1))
         ps = ctx.enter_context(tc.psum_pool(name="ps", bufs=1))
 
         offsets = sb.tile([P, SLOTS // 16], U16, name="offsets")
@@ -34,50 +33,48 @@ def tile_attend_plh_reglu_topk_kernel(tc, qT, k_words, k_scales, c_words, c_scal
         k_bytes = sb.tile([P, POOL], U8, name="k_bytes", align_bytes=64)
         c_pool = sb.tile([P, POOL], I32, name="c_pool", align_bytes=64)
         k_pool = sb.tile([P, POOL], I32, name="k_pool", align_bytes=64)
-        q_raw = reused.tile([P, PACK, NQ], F32, name="q_raw", offset=0, align_bytes=64)
+        q_raw = sb.tile([P, PACK, NQ], F32, name="q_raw", align_bytes=64)
+
+        c_plane = sb.tile([P, SLOTS], U8, name="c_plane", align_bytes=64)
+        k_plane = sb.tile([P, SLOTS], U8, name="k_plane", align_bytes=64)
 
         nc.vector.memset(k_bytes[:].bitcast(I32), 0)
         nc.vector.memset(c_bytes[:].bitcast(I32)[:96, :], 0)
-        nc.vector.memset(c_bytes[:].bitcast(I32)[96:FIRST_ROW, :], 0)
+        nc.vector.memset(c_bytes[:].bitcast(I32)[96:C_ROW, :], 0)
+        nc.vector.memset(c_plane[:].bitcast(I32), 0)
         nc.sync.dma_start(offsets[:], offs)
 
         def load_words(tile, words):
             nc.sync.dma_start(tile[:], words[0].rearrange("p t r -> p (t r)").bitcast(I32))
 
-        nc.scalar.dma_start(c_bytes[:].bitcast(I32)[FIRST_ROW:, :], c_scales[0].bitcast(I32))
+        nc.scalar.dma_start(c_bytes[:].bitcast(I32)[C_ROW:, :], c_scales[0].bitcast(I32))
         nc.sync.dma_start(q_raw[:], qT[0].rearrange("(p j) q -> p j q", j=PACK))
         nc.sync.dma_start(k_bytes[:].bitcast(I32)[0:P:ROW_STEP, :], k_scales[0].bitcast(I32))
         load_words(c_pool, c_words)
         load_words(k_pool, k_words)
 
         def gather_scales(name, window):
-            listed = sb.tile([P, SLOTS], U8, name=name, align_bytes=64)
-            nc.vector.tensor_copy(listed[:], window[:].indirect(offsets[:]))
-            return listed
-
-        def deal_scales(dealt, listed):
-            nc.vector.tensor_copy(dealt.rearrange("p (r s) -> p r s", r=PACK), listed[:].rearrange("p (s r) -> p r s", r=PACK))
+            dealt = sb.tile([P, SLOTS], U8, name=name, align_bytes=64)
+            nc.vector.tensor_copy(dealt[:].rearrange("p (r s) -> p s r", r=PACK), window[:].indirect(offsets[:]))
+            return dealt
 
         def gather_words(name, window, tag):
             dealt = sb.tile([P, SLOTS], U32, name=name, tag=tag, align_bytes=64)
             nc.vector.tensor_copy(dealt[:].rearrange("p (r s) -> p s r", r=PACK), window[:].bitcast(U32).indirect(offsets[:]))
             return dealt
 
-        c_listed = gather_scales("c_listed", c_bytes)
-        k_listed = gather_scales("k_listed", k_bytes)
+        c_sc = c_plane[:]
+        k_sc = k_plane[:]
+        c_dealt = gather_scales("c_dealt", c_bytes)
+        for i in range(4):
+            nc.sync.dma_start(c_sc.bitcast(I32)[i:P:32, :], c_dealt[:].bitcast(I32)[C_ROW + i : P : 4, :])
+        k_dealt = gather_scales("k_dealt", k_bytes)
+        nc.vector.tensor_copy(k_sc.bitcast(I32), k_dealt[:].bitcast(I32))
+        for i in range(1, 4):
+            nc.sync.dma_start(k_sc.bitcast(I32)[i:P:32, :], k_dealt[:].bitcast(I32)[ROW_STEP * i : P : 32, :])
 
         q_bf = sb.tile([P, NQ, PACK], BF16, name="q_bf", tag="q_bf", align_bytes=64)
         nc.scalar.copy(q_bf[:].rearrange("p (c i) t -> p c t i", i=4), q_raw[:].rearrange("p t (c i) -> p c t i", i=4))
-        c_plane = reused.tile([P, SLOTS], U8, name="c_plane", offset=0, align_bytes=64)
-        k_plane = reused.tile([P, SLOTS], U8, name="k_plane", offset=SLOTS, align_bytes=64)
-        c_sc = c_plane[:]
-        k_sc = k_plane[:]
-        deal_scales(c_sc, c_listed)
-        for i in range(4):
-            nc.sync.dma_start(c_sc.bitcast(I32)[i:P:32, :], c_sc.bitcast(I32)[FIRST_ROW + i : P : 4, :])
-        deal_scales(k_sc, k_listed)
-        for i in range(1, 4):
-            nc.sync.dma_start(k_sc.bitcast(I32)[i:P:32, :], k_sc.bitcast(I32)[ROW_STEP * i : P : 32, :])
         q_codes = sb.tile([P, NQ], U32, name="q_codes", align_bytes=64)
         q_sc = sb.tile([P, NQ], U8, name="q_sc", align_bytes=64)
         nc.vector.quantize_mx(out=q_codes[:].bitcast(FP8X4), scales=q_sc[:], in_=q_bf[:].rearrange("p q t -> p (q t)"))

@@ -18,6 +18,7 @@ P = 128
 PACK = 4
 HALF = NQ // 2
 ROWS = 16
+SCALAR_RUNS = (20, 8)
 C_ROW = P - ROWS
 ROW_STEP = P // ROWS
 
@@ -82,45 +83,46 @@ def tile_attend_plh_reglu_topk_kernel(tc, qT, k_words, k_scales, c_words, c_scal
         c_cols = gather_words("c_cols", c_pool, "c_cols")
         k_cols = gather_words("k_cols", k_pool, "k_cols")
 
-        z_sb = sb.tile([P, 2, PACK, HALF], F32, name="z_sb", align_bytes=64)
-        for h in range(2):
-            qs = slice(h * HALF, (h + 1) * HALF)
-            for pair in range(2):
-                bank = ps.tile([P, 2, HALF], F32, name=f"z_bank{h}{pair}", tag=f"bank{h}{pair}")
-                for i in range(2):
-                    cols = slice((2 * pair + i) * P, (2 * pair + i + 1) * P)
-                    nc.tensor.matmul_mx(out=bank[:, i, :], lhsT=c_cols[:, cols].bitcast(FP8X4), lhsT_scale=c_sc[:, cols],
-                                        rhs=q_codes[:, qs].bitcast(FP8X4), rhs_scale=q_sc[:, qs], start=True, stop=True)
-                nc.scalar.copy(z_sb[:, h, 2 * pair : 2 * pair + 2, :], bank[:])
+        def product(bank, words, plane, r, qs):
+            cols = slice(r * P, (r + 1) * P)
+            nc.tensor.matmul_mx(out=bank, lhsT=words[:, cols].bitcast(FP8X4), lhsT_scale=plane[:, cols],
+                                rhs=q_codes[:, qs].bitcast(FP8X4), rhs_scale=q_sc[:, qs], start=True, stop=True)
+
+        halves = [slice(0, HALF), slice(HALF, NQ)]
+        pieces = [([0], slice(0, NQ)), ([1], slice(0, NQ)), ([2, 3], halves[0]), ([2, 3], halves[1])]
+
+        def products(name, piece, words, plane):
+            rows, qs = pieces[piece]
+            bank = ps.tile([P, len(rows), NQ // len(rows)], F32, name=f"{name}{piece}", tag=f"bank{piece}")
+            for i, r in enumerate(rows):
+                product(bank[:, i, :], words, plane, r, qs)
+            return bank, slice(rows[0], rows[-1] + 1), qs
+
+        z_sb = sb.tile([P, PACK, NQ], F32, name="z_sb", align_bytes=64)
+        for piece in range(4):
+            bank, rs, qs = products("z_bank", piece, c_cols, c_sc)
+            nc.scalar.copy(z_sb[:, rs, qs], bank[:])
 
         y_codes = sb.tile([P, NQ], U32, name="y_codes", align_bytes=64)
         y_sc = sb.tile([P, NQ], U8, name="y_sc", align_bytes=64)
         out_rows = out_0.rearrange("(p r) q -> p r q", r=PACK)
         out_words = out_1[0].rearrange("p q u -> p (q u)").bitcast(I32)
         y = sb.tile([P, PACK, NQ], F32, name="y", align_bytes=64)
+        for piece in range(4):
+            bank, rs, qs = products("a_bank", piece, k_cols, k_sc)
+            nc.vector.scalar_tensor_tensor(out=y[:, rs, qs], in0=bank[:], scalar=0.0, in1=z_sb[:, rs, qs], op0=ALU.max, op1=ALU.mult)
+            if piece % 2:
+                nc.sync.dma_start(out_rows[:, piece - 1 : piece + 1, :], y[:, piece - 1 : piece + 1, :])
+        y_bf = [sb.tile([P, HALF, PACK], BF16, name=f"y_bf{h}", align_bytes=64) for h in range(2)]
         for h in range(2):
-            qs = slice(h * HALF, (h + 1) * HALF)
-            for pair in range(2):
-                bank = ps.tile([P, 2, HALF], F32, name=f"a_bank{h}{pair}", tag=f"bank{h}{pair}")
-                for i in range(2):
-                    cols = slice((2 * pair + i) * P, (2 * pair + i + 1) * P)
-                    nc.tensor.matmul_mx(out=bank[:, i, :], lhsT=k_cols[:, cols].bitcast(FP8X4), lhsT_scale=k_sc[:, cols],
-                                        rhs=q_codes[:, qs].bitcast(FP8X4), rhs_scale=q_sc[:, qs], start=True, stop=True)
-                rs = slice(2 * pair, 2 * pair + 2)
-                nc.vector.scalar_tensor_tensor(out=y[:, rs, qs], in0=bank[:], scalar=0.0, in1=z_sb[:, h, rs, :], op0=ALU.max, op1=ALU.mult)
-                if h == 1:
-                    nc.sync.dma_start(out_rows[:, rs, :], y[:, rs, :])
+            dst = y_bf[h][:].rearrange("p (c i) t -> p c t i", i=4)
+            src = y[:, :, halves[h]].rearrange("p t (c i) -> p c t i", i=4)
+            n = SCALAR_RUNS[h]
+            nc.scalar.copy(dst[:, :n], src[:, :n])
+            nc.vector.tensor_copy(dst[:, n:], src[:, n:])
         for h in range(2):
-            qs = slice(h * HALF, (h + 1) * HALF)
-            y_bf = sb.tile([P, HALF, PACK], BF16, name=f"y_bf{h}", align_bytes=64)
-            dst = y_bf[:].rearrange("p (c i) t -> p c t i", i=4)
-            src = y[:, :, qs].rearrange("p t (c i) -> p c t i", i=4)
-            if h == 0:
-                nc.scalar.copy(dst, src)
-            else:
-                nc.scalar.copy(dst[:, :16], src[:, :16])
-                nc.vector.tensor_copy(dst[:, 16:], src[:, 16:])
-            nc.vector.quantize_mx(out=y_codes[:, qs].bitcast(FP8X4), scales=y_sc[:, qs], in_=y_bf[:].rearrange("p q t -> p (q t)"))
+            qs = halves[h]
+            nc.vector.quantize_mx(out=y_codes[:, qs].bitcast(FP8X4), scales=y_sc[:, qs], in_=y_bf[h][:].rearrange("p q t -> p (q t)"))
             nc.sync.dma_start(out_words[:, qs], y_codes[:, qs].bitcast(I32))
         for quadrant in range(4):
             queue = nc.scalar if quadrant % 2 else nc.sync

@@ -43,13 +43,13 @@ def tile_attend_plh_reglu_topk_kernel(tc, qT, k_words, k_scales, c_words, c_scal
         nc.vector.memset(c_bytes[:].bitcast(I32)[:96, :], 0)
         nc.vector.memset(c_bytes[:].bitcast(I32)[96:C_ROW, :], 0)
         nc.vector.memset(c_plane[:].bitcast(I32), 0)
-        nc.sync.dma_start(offsets[:], offs)
 
         def load_words(tile, words):
             nc.sync.dma_start(tile[:], words[0].rearrange("p t r -> p (t r)").bitcast(I32))
 
         nc.scalar.dma_start(c_bytes[:].bitcast(I32)[C_ROW:, :], c_scales[0].bitcast(I32))
         nc.sync.dma_start(q_raw[:], qT[0].rearrange("(p j) q -> p j q", j=PACK))
+        nc.sync.dma_start(offsets[:], offs)
         nc.sync.dma_start(k_bytes[:].bitcast(I32)[0:P:ROW_STEP, :], k_scales[0].bitcast(I32))
         load_words(c_pool, c_words)
         load_words(k_pool, k_words)
@@ -70,15 +70,15 @@ def tile_attend_plh_reglu_topk_kernel(tc, qT, k_words, k_scales, c_words, c_scal
         for i in range(4):
             nc.sync.dma_start(c_sc.bitcast(I32)[i:P:32, :], c_dealt[:].bitcast(I32)[C_ROW + i : P : 4, :])
         k_dealt = gather_scales("k_dealt", k_bytes)
-        nc.vector.tensor_copy(k_sc.bitcast(I32), k_dealt[:].bitcast(I32))
-        for i in range(1, 4):
-            nc.sync.dma_start(k_sc.bitcast(I32)[i:P:32, :], k_dealt[:].bitcast(I32)[ROW_STEP * i : P : 32, :])
 
         q_bf = sb.tile([P, NQ, PACK], BF16, name="q_bf", tag="q_bf", align_bytes=64)
         nc.scalar.copy(q_bf[:].rearrange("p (c i) t -> p c t i", i=4), q_raw[:].rearrange("p t (c i) -> p c t i", i=4))
         q_codes = sb.tile([P, NQ], U32, name="q_codes", align_bytes=64)
         q_sc = sb.tile([P, NQ], U8, name="q_sc", align_bytes=64)
         nc.vector.quantize_mx(out=q_codes[:].bitcast(FP8X4), scales=q_sc[:], in_=q_bf[:].rearrange("p q t -> p (q t)"))
+        nc.vector.tensor_copy(k_sc.bitcast(I32), k_dealt[:].bitcast(I32))
+        for i in range(1, 4):
+            nc.sync.dma_start(k_sc.bitcast(I32)[i:P:32, :], k_dealt[:].bitcast(I32)[ROW_STEP * i : P : 32, :])
 
         c_cols = gather_words("c_cols", c_pool, "c_cols")
         k_cols = gather_words("k_cols", k_pool, "k_cols")

@@ -18,7 +18,7 @@ P = 128
 PACK = 4
 HALF = NQ // 2
 ROWS = 16
-SCALAR_RUNS = (20, 8)
+QUARTER = NQ // 4
 C_ROW = P - ROWS
 ROW_STEP = P // ROWS
 
@@ -29,101 +29,114 @@ def tile_attend_plh_reglu_topk_kernel(tc, qT, k_words, k_scales, c_words, c_scal
         sb = ctx.enter_context(tc.tile_pool(name="sb", bufs=1))
         ps = ctx.enter_context(tc.psum_pool(name="ps", bufs=1))
 
-        offsets = sb.tile([P, SLOTS // 16], U16, name="offsets")
-        c_bytes = sb.tile([P, POOL], U8, name="c_bytes", align_bytes=64)
-        k_bytes = sb.tile([P, POOL], U8, name="k_bytes", align_bytes=64)
-        c_pool = sb.tile([P, POOL], I32, name="c_pool", align_bytes=64)
-        k_pool = sb.tile([P, POOL], I32, name="k_pool", align_bytes=64)
-        q_raw = sb.tile([P, PACK, NQ], F32, name="q_raw", align_bytes=64)
+        def sbuf(name, shape, dtype):
+            return sb.tile(shape, dtype, name=name, align_bytes=64)
 
-        c_plane = sb.tile([P, SLOTS], U8, name="c_plane", align_bytes=64)
-        k_plane = sb.tile([P, SLOTS], U8, name="k_plane", align_bytes=64)
+        offsets = sb.tile([P, SLOTS // 16], U16, name="offsets")
+        c_bytes = sbuf("c_bytes", [P, POOL], U8)
+        k_bytes = sbuf("k_bytes", [P, POOL], U8)
+        c_pool = sbuf("c_pool", [P, POOL], I32)
+        k_pool = sbuf("k_pool", [P, POOL], I32)
+        q_raw = sbuf("q_raw", [P, PACK, NQ], F32)
+        c_plane = sbuf("c_plane", [P, SLOTS], U8)
+        k_plane = sbuf("k_plane", [P, SLOTS], U8)
 
         nc.vector.memset(k_bytes[:].bitcast(I32), 0)
         nc.vector.memset(c_bytes[:].bitcast(I32)[:96, :], 0)
         nc.vector.memset(c_bytes[:].bitcast(I32)[96:C_ROW, :], 0)
         nc.vector.memset(c_plane[:].bitcast(I32), 0)
 
-        def load_words(tile, words):
-            nc.sync.dma_start(tile[:], words[0].rearrange("p t r -> p (t r)").bitcast(I32))
-
         nc.scalar.dma_start(c_bytes[:].bitcast(I32)[C_ROW:, :], c_scales[0].bitcast(I32))
         nc.sync.dma_start(q_raw[:], qT[0].rearrange("(p j) q -> p j q", j=PACK))
         nc.sync.dma_start(offsets[:], offs)
         nc.sync.dma_start(k_bytes[:].bitcast(I32)[0:P:ROW_STEP, :], k_scales[0].bitcast(I32))
-        load_words(c_pool, c_words)
-        load_words(k_pool, k_words)
+        for pool, words in ((c_pool, c_words), (k_pool, k_words)):
+            nc.sync.dma_start(pool[:], words[0].rearrange("p t r -> p (t r)").bitcast(I32))
 
-        def gather_scales(name, window):
-            dealt = sb.tile([P, SLOTS], U8, name=name, align_bytes=64)
-            nc.vector.tensor_copy(dealt[:].rearrange("p (r s) -> p s r", r=PACK), window[:].indirect(offsets[:]))
+        def gather(name, window, dtype):
+            dealt = sbuf(name, [P, SLOTS], dtype)
+            nc.vector.tensor_copy(dealt[:].rearrange("p (r s) -> p s r", r=PACK), window.indirect(offsets[:]))
             return dealt
 
-        def gather_words(name, window, tag):
-            dealt = sb.tile([P, SLOTS], U32, name=name, tag=tag, align_bytes=64)
-            nc.vector.tensor_copy(dealt[:].rearrange("p (r s) -> p s r", r=PACK), window[:].bitcast(U32).indirect(offsets[:]))
-            return dealt
-
-        c_sc = c_plane[:]
-        k_sc = k_plane[:]
-        c_dealt = gather_scales("c_dealt", c_bytes)
+        c_dealt = gather("c_dealt", c_bytes[:], U8)
         for i in range(4):
-            nc.sync.dma_start(c_sc.bitcast(I32)[i:P:32, :], c_dealt[:].bitcast(I32)[C_ROW + i : P : 4, :])
-        k_dealt = gather_scales("k_dealt", k_bytes)
+            nc.sync.dma_start(c_plane[:].bitcast(I32)[i:P:32, :], c_dealt[:].bitcast(I32)[C_ROW + i : P : 4, :])
+        k_dealt = gather("k_dealt", k_bytes[:], U8)
 
-        q_bf = sb.tile([P, NQ, PACK], BF16, name="q_bf", tag="q_bf", align_bytes=64)
+        q_bf = sbuf("q_bf", [P, NQ, PACK], BF16)
         nc.scalar.copy(q_bf[:].rearrange("p (c i) t -> p c t i", i=4), q_raw[:].rearrange("p t (c i) -> p c t i", i=4))
-        q_codes = sb.tile([P, NQ], U32, name="q_codes", align_bytes=64)
-        q_sc = sb.tile([P, NQ], U8, name="q_sc", align_bytes=64)
+        q_codes = sbuf("q_codes", [P, NQ], U32)
+        q_sc = sbuf("q_sc", [P, NQ], U8)
         nc.vector.quantize_mx(out=q_codes[:].bitcast(FP8X4), scales=q_sc[:], in_=q_bf[:].rearrange("p q t -> p (q t)"))
-        nc.vector.tensor_copy(k_sc.bitcast(I32), k_dealt[:].bitcast(I32))
+        nc.vector.tensor_copy(k_plane[:].bitcast(I32), k_dealt[:].bitcast(I32))
         for i in range(1, 4):
-            nc.sync.dma_start(k_sc.bitcast(I32)[i:P:32, :], k_dealt[:].bitcast(I32)[ROW_STEP * i : P : 32, :])
+            nc.sync.dma_start(k_plane[:].bitcast(I32)[i:P:32, :], k_dealt[:].bitcast(I32)[ROW_STEP * i : P : 32, :])
 
-        c_cols = gather_words("c_cols", c_pool, "c_cols")
-        k_cols = gather_words("k_cols", k_pool, "k_cols")
+        c_cols = gather("c_cols", c_pool[:].bitcast(U32), U32)
+        k_cols = gather("k_cols", k_pool[:].bitcast(U32), U32)
 
-        def product(bank, words, plane, r, qs):
-            cols = slice(r * P, (r + 1) * P)
-            nc.tensor.matmul_mx(out=bank, lhsT=words[:, cols].bitcast(FP8X4), lhsT_scale=plane[:, cols],
-                                rhs=q_codes[:, qs].bitcast(FP8X4), rhs_scale=q_sc[:, qs], start=True, stop=True)
+        every, low, high = slice(0, NQ), slice(0, HALF), slice(HALF, NQ)
+        z_sb = sbuf("z_sb", [P, PACK, NQ], F32)
+        y = sbuf("y", [P, PACK, NQ], F32)
 
-        halves = [slice(0, HALF), slice(HALF, NQ)]
-        pieces = [([0], slice(0, NQ)), ([1], slice(0, NQ)), ([2, 3], halves[0]), ([2, 3], halves[1])]
+        def products(name, bank_no, words, plane, rows, qs):
+            bank = ps.tile([P, rows.stop - rows.start, qs.stop - qs.start], F32, name=name, tag=f"bank{bank_no}")
+            for r in range(rows.start, rows.stop):
+                cols = slice(r * P, (r + 1) * P)
+                nc.tensor.matmul_mx(out=bank[:, r - rows.start, :], lhsT=words[:, cols].bitcast(FP8X4), lhsT_scale=plane[:, cols],
+                                    rhs=q_codes[:, qs].bitcast(FP8X4), rhs_scale=q_sc[:, qs], start=True, stop=True)
+            return bank
 
-        def products(name, piece, words, plane):
-            rows, qs = pieces[piece]
-            bank = ps.tile([P, len(rows), NQ // len(rows)], F32, name=f"{name}{piece}", tag=f"bank{piece}")
-            for i, r in enumerate(rows):
-                product(bank[:, i, :], words, plane, r, qs)
-            return bank, slice(rows[0], rows[-1] + 1), qs
+        def layer(name, bank_no, rows, qs):
+            bank = products(name, bank_no, c_cols, c_plane, rows, qs)
+            nc.scalar.copy(z_sb[:, rows, qs], bank[:])
 
-        z_sb = sb.tile([P, PACK, NQ], F32, name="z_sb", align_bytes=64)
-        for piece in range(4):
-            bank, rs, qs = products("z_bank", piece, c_cols, c_sc)
-            nc.scalar.copy(z_sb[:, rs, qs], bank[:])
+        def gate_products(name, bank_no, rows, qs):
+            return products(name, bank_no, k_cols, k_plane, rows, qs)[:], rows, qs
 
-        y_codes = sb.tile([P, NQ], U32, name="y_codes", align_bytes=64)
-        y_sc = sb.tile([P, NQ], U8, name="y_sc", align_bytes=64)
+        def gate(piece):
+            bank, rows, qs = piece
+            nc.vector.scalar_tensor_tensor(out=y[:, rows, qs], in0=bank, scalar=0.0, in1=z_sb[:, rows, qs], op0=ALU.max, op1=ALU.mult)
+
         out_rows = out_0.rearrange("(p r) q -> p r q", r=PACK)
         out_words = out_1[0].rearrange("p q u -> p (q u)").bitcast(I32)
-        y = sb.tile([P, PACK, NQ], F32, name="y", align_bytes=64)
-        for piece in range(4):
-            bank, rs, qs = products("a_bank", piece, k_cols, k_sc)
-            nc.vector.scalar_tensor_tensor(out=y[:, rs, qs], in0=bank[:], scalar=0.0, in1=z_sb[:, rs, qs], op0=ALU.max, op1=ALU.mult)
-            if piece % 2:
-                nc.sync.dma_start(out_rows[:, piece - 1 : piece + 1, :], y[:, piece - 1 : piece + 1, :])
-        y_bf = [sb.tile([P, HALF, PACK], BF16, name=f"y_bf{h}", align_bytes=64) for h in range(2)]
-        for h in range(2):
-            dst = y_bf[h][:].rearrange("p (c i) t -> p c t i", i=4)
-            src = y[:, :, halves[h]].rearrange("p t (c i) -> p c t i", i=4)
-            n = SCALAR_RUNS[h]
-            nc.scalar.copy(dst[:, :n], src[:, :n])
-            nc.vector.tensor_copy(dst[:, n:], src[:, n:])
-        for h in range(2):
-            qs = halves[h]
-            nc.vector.quantize_mx(out=y_codes[:, qs].bitcast(FP8X4), scales=y_sc[:, qs], in_=y_bf[h][:].rearrange("p q t -> p (q t)"))
-            nc.sync.dma_start(out_words[:, qs], y_codes[:, qs].bitcast(I32))
+
+        third, fourth = slice(HALF, HALF + QUARTER), slice(HALF + QUARTER, NQ)
+        for r in range(PACK):
+            layer(f"z{r}", r, slice(r, r + 1), every)
+        for r in range(PACK):
+            gate(gate_products(f"a{r}_low", PACK + r, slice(r, r + 1), low))
+        nc.sync.dma_start(out_rows[:, :, low], y[:, :, low])
+        for r in range(PACK - 1):
+            gate(gate_products(f"a{r}_high", r, slice(r, r + 1), high))
+        last, rows, qs = gate_products("a3_high", PACK - 1, slice(PACK - 1, PACK), high)
+        gate((last[:, :, :QUARTER], rows, third))
+        gate((last[:, :, QUARTER:], rows, fourth))
+        nc.sync.dma_start(out_rows[:, :, high], y[:, :, high])
+
+        y_codes = sbuf("y_codes", [P, NQ], U32)
+        y_sc = sbuf("y_sc", [P, NQ], U8)
+
+        def rounded(name, qs, scalar_runs):
+            y_bf = sbuf(name, [P, qs.stop - qs.start, PACK], BF16)
+            dst = y_bf[:].rearrange("p (c i) t -> p c t i", i=4)
+            src = y[:, :, qs].rearrange("p t (c i) -> p c t i", i=4)
+            if scalar_runs:
+                nc.scalar.copy(dst[:, :scalar_runs], src[:, :scalar_runs])
+            nc.vector.tensor_copy(dst[:, scalar_runs:], src[:, scalar_runs:])
+            return y_bf
+
+        def quantise(y_bf, qs):
+            nc.vector.quantize_mx(out=y_codes[:, qs].bitcast(FP8X4), scales=y_sc[:, qs], in_=y_bf[:].rearrange("p q t -> p (q t)"))
+
+        bf_low = rounded("bf_low", low, 24)
+        bf_third = rounded("bf_third", third, 8)
+        bf_fourth = rounded("bf_fourth", fourth, 0)
+        quantise(bf_low, low)
+        nc.sync.dma_start(out_words[:, low], y_codes[:, low].bitcast(I32))
+        quantise(bf_third, third)
+        quantise(bf_fourth, fourth)
+        nc.sync.dma_start(out_words[:, high], y_codes[:, high].bitcast(I32))
         for quadrant in range(4):
             queue = nc.scalar if quadrant % 2 else nc.sync
             queue.dma_start(out_2[0, 4 * quadrant : 4 * quadrant + 4, :].bitcast(I32), y_sc[32 * quadrant : 32 * quadrant + 4, :].bitcast(I32))

@@ -104,15 +104,15 @@ def tile_attend_plh_reglu_topk_kernel(tc, qT, k_words, k_scales, c_words, c_scal
         third, fourth = slice(HALF, HALF + QUARTER), slice(HALF + QUARTER, NQ)
         for r in range(PACK):
             layer(f"z{r}", r, slice(r, r + 1), every)
-        for r in range(PACK):
-            gate(gate_products(f"a{r}_low", PACK + r, slice(r, r + 1), low))
-        nc.sync.dma_start(out_rows[:, :, low], y[:, :, low])
-        for r in range(PACK - 1):
-            gate(gate_products(f"a{r}_high", r, slice(r, r + 1), high))
+        order = [(0, low), (0, high), (1, low), (1, high), (2, low), (3, low), (2, high)]
+        for i, (r, qs) in enumerate(order):
+            gate(gate_products(f"a{i}", (PACK + i) % 8, slice(r, r + 1), qs))
+            if i == 3:
+                nc.sync.dma_start(out_rows[:, 0:2, :], y[:, 0:2, :])
         last, rows, qs = gate_products("a3_high", PACK - 1, slice(PACK - 1, PACK), high)
         gate((last[:, :, :QUARTER], rows, third))
         gate((last[:, :, QUARTER:], rows, fourth))
-        nc.sync.dma_start(out_rows[:, :, high], y[:, :, high])
+        nc.sync.dma_start(out_rows[:, 2:4, :], y[:, 2:4, :])
 
         y_codes = sbuf("y_codes", [P, NQ], U32)
         y_sc = sbuf("y_sc", [P, NQ], U8)
@@ -129,8 +129,8 @@ def tile_attend_plh_reglu_topk_kernel(tc, qT, k_words, k_scales, c_words, c_scal
         def quantise(y_bf, qs):
             nc.vector.quantize_mx(out=y_codes[:, qs].bitcast(FP8X4), scales=y_sc[:, qs], in_=y_bf[:].rearrange("p q t -> p (q t)"))
 
-        bf_low = rounded("bf_low", low, 24)
-        bf_third = rounded("bf_third", third, 8)
+        bf_low = rounded("bf_low", low, 16)
+        bf_third = rounded("bf_third", third, 6)
         bf_fourth = rounded("bf_fourth", fourth, 0)
         quantise(bf_low, low)
         nc.sync.dma_start(out_words[:, low], y_codes[:, low].bitcast(I32))

@@ -133,10 +133,9 @@ def tile_attend_plh_reglu_topk_kernel(tc, qT, k_words, k_scales, c_words, c_scal
         bf_third = rounded("bf_third", third, 6)
         bf_fourth = rounded("bf_fourth", fourth, 0)
         quantise(bf_low, low)
-        nc.sync.dma_start(out_words[:, low], y_codes[:, low].bitcast(I32))
         quantise(bf_third, third)
         quantise(bf_fourth, fourth)
-        nc.sync.dma_start(out_words[:, high], y_codes[:, high].bitcast(I32))
+        nc.sync.dma_start(out_words, y_codes[:].bitcast(I32))
         for quadrant in range(4):
             queue = nc.scalar if quadrant % 2 else nc.sync
             queue.dma_start(out_2[0, 4 * quadrant : 4 * quadrant + 4, :].bitcast(I32), y_sc[32 * quadrant : 32 * quadrant + 4, :].bitcast(I32))

@@ -19,6 +19,7 @@ PACK = 4
 HALF = NQ // 2
 ROWS = 16
 QUARTER = NQ // 4
+WORDS_RUN = P * NQ * PACK // 16
 C_ROW = P - ROWS
 ROW_STEP = P // ROWS
 
@@ -104,11 +105,11 @@ def tile_attend_plh_reglu_topk_kernel(tc, qT, k_words, k_scales, c_words, c_scal
         third, fourth = slice(HALF, HALF + QUARTER), slice(HALF + QUARTER, NQ)
         for r in range(PACK):
             layer(f"z{r}", r, slice(r, r + 1), every)
-        order = [(0, low), (0, high), (1, low), (1, high), (2, low), (3, low), (2, high)]
+        order = [(0, low), (0, high), (1, low), (2, low), (3, low), (1, high), (2, high)]
         for i, (r, qs) in enumerate(order):
             gate(gate_products(f"a{i}", (PACK + i) % 8, slice(r, r + 1), qs))
-            if i == 3:
-                nc.sync.dma_start(out_rows[:, 0:2, :], y[:, 0:2, :])
+            if qs == high and r < 2:
+                nc.sync.dma_start(out_rows[:, r, :], y[:, r, :])
         last, rows, qs = gate_products("a3_high", PACK - 1, slice(PACK - 1, PACK), high)
         gate((last[:, :, :QUARTER], rows, third))
         gate((last[:, :, QUARTER:], rows, fourth))
@@ -129,13 +130,13 @@ def tile_attend_plh_reglu_topk_kernel(tc, qT, k_words, k_scales, c_words, c_scal
         def quantise(y_bf, qs):
             nc.vector.quantize_mx(out=y_codes[:, qs].bitcast(FP8X4), scales=y_sc[:, qs], in_=y_bf[:].rearrange("p q t -> p (q t)"))
 
-        bf_low = rounded("bf_low", low, 16)
+        bf_low = rounded("bf_low", low, 24)
         bf_third = rounded("bf_third", third, 6)
         bf_fourth = rounded("bf_fourth", fourth, 0)
         quantise(bf_low, low)
         quantise(bf_third, third)
         quantise(bf_fourth, fourth)
-        nc.sync.dma_start(out_words, y_codes[:].bitcast(I32))
-        for quadrant in range(4):
-            queue = nc.scalar if quadrant % 2 else nc.sync
-            queue.dma_start(out_2[0, 4 * quadrant : 4 * quadrant + 4, :].bitcast(I32), y_sc[32 * quadrant : 32 * quadrant + 4, :].bitcast(I32))
+        nc.sync.dma_start(out_words, y_codes[:].bitcast(I32), max_dma_last_dim=WORDS_RUN)
+        for i in range(4):
+            queue = nc.scalar if i % 2 else nc.sync
+            queue.dma_start(out_2[0, i:ROWS:4, :].bitcast(I32), y_sc[i:P:32, :].bitcast(I32))

@@ -20,7 +20,7 @@ HALF = NQ // 2
 ROWS = 16
 QUARTER = NQ // 4
 WORDS_RUN = P * NQ * PACK // 16
-C_ROW = P - ROWS
+K_FIRST = 4
 ROW_STEP = P // ROWS
 
 
@@ -42,15 +42,13 @@ def tile_attend_plh_reglu_topk_kernel(tc, qT, k_words, k_scales, c_words, c_scal
         c_plane = sbuf("c_plane", [P, SLOTS], U8)
         k_plane = sbuf("k_plane", [P, SLOTS], U8)
 
+        nc.vector.memset(c_bytes[:].bitcast(I32), 0)
         nc.vector.memset(k_bytes[:].bitcast(I32), 0)
-        nc.vector.memset(c_bytes[:].bitcast(I32)[:96, :], 0)
-        nc.vector.memset(c_bytes[:].bitcast(I32)[96:C_ROW, :], 0)
-        nc.vector.memset(c_plane[:].bitcast(I32), 0)
 
-        nc.scalar.dma_start(c_bytes[:].bitcast(I32)[C_ROW:, :], c_scales[0].bitcast(I32))
         nc.sync.dma_start(q_raw[:], qT[0].rearrange("(p j) q -> p j q", j=PACK))
         nc.sync.dma_start(offsets[:], offs)
-        nc.sync.dma_start(k_bytes[:].bitcast(I32)[0:P:ROW_STEP, :], k_scales[0].bitcast(I32))
+        nc.sync.dma_start(c_bytes[:].bitcast(I32)[0:P:ROW_STEP, :], c_scales[0].bitcast(I32))
+        nc.sync.dma_start(k_bytes[:].bitcast(I32)[K_FIRST:P:ROW_STEP, :], k_scales[0].bitcast(I32))
         for pool, words in ((c_pool, c_words), (k_pool, k_words)):
             nc.sync.dma_start(pool[:], words[0].rearrange("p t r -> p (t r)").bitcast(I32))
 
@@ -59,19 +57,21 @@ def tile_attend_plh_reglu_topk_kernel(tc, qT, k_words, k_scales, c_words, c_scal
             nc.vector.tensor_copy(dealt[:].rearrange("p (r s) -> p s r", r=PACK), window.indirect(offsets[:]))
             return dealt
 
+        def place(plane, dealt, first):
+            nc.vector.tensor_copy(plane[:].bitcast(I32), dealt[:].bitcast(I32))
+            for i in range(1, 4):
+                nc.sync.dma_start(plane[:].bitcast(I32)[first + i : P : 32, :], dealt[:].bitcast(I32)[first + ROW_STEP * i : P : 32, :])
+
         c_dealt = gather("c_dealt", c_bytes[:], U8)
-        for i in range(4):
-            nc.sync.dma_start(c_plane[:].bitcast(I32)[i:P:32, :], c_dealt[:].bitcast(I32)[C_ROW + i : P : 4, :])
         k_dealt = gather("k_dealt", k_bytes[:], U8)
+        place(c_plane, c_dealt, 0)
 
         q_bf = sbuf("q_bf", [P, NQ, PACK], BF16)
         nc.scalar.copy(q_bf[:].rearrange("p (c i) t -> p c t i", i=4), q_raw[:].rearrange("p t (c i) -> p c t i", i=4))
         q_codes = sbuf("q_codes", [P, NQ], U32)
         q_sc = sbuf("q_sc", [P, NQ], U8)
         nc.vector.quantize_mx(out=q_codes[:].bitcast(FP8X4), scales=q_sc[:], in_=q_bf[:].rearrange("p q t -> p (q t)"))
-        nc.vector.tensor_copy(k_plane[:].bitcast(I32), k_dealt[:].bitcast(I32))
-        for i in range(1, 4):
-            nc.sync.dma_start(k_plane[:].bitcast(I32)[i:P:32, :], k_dealt[:].bitcast(I32)[ROW_STEP * i : P : 32, :])
+        place(k_plane, k_dealt, K_FIRST)
 
         c_cols = gather("c_cols", c_pool[:].bitcast(U32), U32)
         k_cols = gather("k_cols", k_pool[:].bitcast(U32), U32)
@@ -89,11 +89,11 @@ def tile_attend_plh_reglu_topk_kernel(tc, qT, k_words, k_scales, c_words, c_scal
             return bank
 
         def layer(name, bank_no, rows, qs):
-            bank = products(name, bank_no, c_cols, c_plane, rows, qs)
+            bank = products(name, bank_no, c_cols, c_plane[:], rows, qs)
             nc.scalar.copy(z_sb[:, rows, qs], bank[:])
 
         def gate_products(name, bank_no, rows, qs):
-            return products(name, bank_no, k_cols, k_plane, rows, qs)[:], rows, qs
+            return products(name, bank_no, k_cols, k_plane[K_FIRST:, :], rows, qs)[:], rows, qs
 
         def gate(piece):
             bank, rows, qs = piece
@@ -138,5 +138,4 @@ def tile_attend_plh_reglu_topk_kernel(tc, qT, k_words, k_scales, c_words, c_scal
         quantise(bf_fourth, fourth)
         nc.sync.dma_start(out_words, y_codes[:].bitcast(I32), max_dma_last_dim=WORDS_RUN)
         for i in range(4):
-            queue = nc.scalar if i % 2 else nc.sync
-            queue.dma_start(out_2[0, i:ROWS:4, :].bitcast(I32), y_sc[i:P:32, :].bitcast(I32))
+            nc.sync.dma_start(out_2[0, i:ROWS:4, :].bitcast(I32), y_sc[i:P:32, :].bitcast(I32))

@@ -19,7 +19,6 @@ PACK = 4
 HALF = NQ // 2
 ROWS = 16
 QUARTER = NQ // 4
-WORDS_RUN = P * NQ * PACK // 16
 K_FIRST = 4
 ROW_STEP = P // ROWS
 
@@ -136,6 +135,7 @@ def tile_attend_plh_reglu_topk_kernel(tc, qT, k_words, k_scales, c_words, c_scal
         quantise(bf_low, low)
         quantise(bf_third, third)
         quantise(bf_fourth, fourth)
-        nc.sync.dma_start(out_words, y_codes[:].bitcast(I32), max_dma_last_dim=WORDS_RUN)
+        nc.sync.dma_start(out_words, y_codes[:].bitcast(I32))
         for i in range(4):
-            nc.sync.dma_start(out_2[0, i:ROWS:4, :].bitcast(I32), y_sc[i:P:32, :].bitcast(I32))
+            queue = nc.scalar if i % 2 else nc.sync
+            queue.dma_start(out_2[0, i:ROWS:4, :].bitcast(I32), y_sc[i:P:32, :].bitcast(I32))

@@ -129,8 +129,8 @@ def tile_attend_plh_reglu_topk_kernel(tc, qT, k_words, k_scales, c_words, c_scal
         def quantise(y_bf, qs):
             nc.vector.quantize_mx(out=y_codes[:, qs].bitcast(FP8X4), scales=y_sc[:, qs], in_=y_bf[:].rearrange("p q t -> p (q t)"))
 
-        bf_low = rounded("bf_low", low, 24)
-        bf_third = rounded("bf_third", third, 6)
+        bf_low = rounded("bf_low", low, 20)
+        bf_third = rounded("bf_third", third, 8)
         bf_fourth = rounded("bf_fourth", fourth, 0)
         quantise(bf_low, low)
         quantise(bf_third, third)

@@ -21,6 +21,7 @@ ROWS = 16
 QUARTER = NQ // 4
 K_FIRST = 4
 ROW_STEP = P // ROWS
+C_FIRST = P - ROWS
 
 
 def tile_attend_plh_reglu_topk_kernel(tc, qT, k_words, k_scales, c_words, c_scales, offs, out_0, out_1, out_2):
@@ -29,48 +30,47 @@ def tile_attend_plh_reglu_topk_kernel(tc, qT, k_words, k_scales, c_words, c_scal
         sb = ctx.enter_context(tc.tile_pool(name="sb", bufs=1))
         ps = ctx.enter_context(tc.psum_pool(name="ps", bufs=1))
 
-        def sbuf(name, shape, dtype):
-            return sb.tile(shape, dtype, name=name, align_bytes=64)
+        def sbuf(name, shape, dtype, tag=""):
+            return sb.tile(shape, dtype, name=name, tag=tag, align_bytes=256)
 
         offsets = sb.tile([P, SLOTS // 16], U16, name="offsets")
-        c_bytes = sbuf("c_bytes", [P, POOL], U8)
+        c_bytes = sbuf("c_bytes", [P, POOL], U8, tag="early_then_gate")
         k_bytes = sbuf("k_bytes", [P, POOL], U8)
         c_pool = sbuf("c_pool", [P, POOL], I32)
-        k_pool = sbuf("k_pool", [P, POOL], I32)
         q_raw = sbuf("q_raw", [P, PACK, NQ], F32)
         c_plane = sbuf("c_plane", [P, SLOTS], U8)
         k_plane = sbuf("k_plane", [P, SLOTS], U8)
 
-        nc.vector.memset(c_bytes[:].bitcast(I32), 0)
         nc.vector.memset(k_bytes[:].bitcast(I32), 0)
+        nc.vector.memset(c_bytes[:].bitcast(I32)[:C_FIRST, :], 0)
+        nc.vector.memset(c_plane[:].bitcast(I32), 0)
 
-        nc.sync.dma_start(q_raw[:], qT[0].rearrange("(p j) q -> p j q", j=PACK))
         nc.sync.dma_start(offsets[:], offs)
-        nc.sync.dma_start(c_bytes[:].bitcast(I32)[0:P:ROW_STEP, :], c_scales[0].bitcast(I32))
+        nc.sync.dma_start(c_bytes[:].bitcast(I32)[C_FIRST:, :], c_scales[0].bitcast(I32))
+        nc.sync.dma_start(q_raw[:], qT[0].rearrange("(p j) q -> p j q", j=PACK))
         nc.sync.dma_start(k_bytes[:].bitcast(I32)[K_FIRST:P:ROW_STEP, :], k_scales[0].bitcast(I32))
-        for pool, words in ((c_pool, c_words), (k_pool, k_words)):
-            nc.sync.dma_start(pool[:], words[0].rearrange("p t r -> p (t r)").bitcast(I32))
+        nc.sync.dma_start(c_pool[:], c_words[0].rearrange("p t r -> p (t r)").bitcast(I32))
 
         def gather(name, window, dtype):
             dealt = sbuf(name, [P, SLOTS], dtype)
             nc.vector.tensor_copy(dealt[:].rearrange("p (r s) -> p s r", r=PACK), window.indirect(offsets[:]))
             return dealt
 
-        def place(plane, dealt, first):
-            nc.vector.tensor_copy(plane[:].bitcast(I32), dealt[:].bitcast(I32))
-            for i in range(1, 4):
-                nc.sync.dma_start(plane[:].bitcast(I32)[first + i : P : 32, :], dealt[:].bitcast(I32)[first + ROW_STEP * i : P : 32, :])
-
         c_dealt = gather("c_dealt", c_bytes[:], U8)
-        k_dealt = gather("k_dealt", k_bytes[:], U8)
-        place(c_plane, c_dealt, 0)
+        for i in range(4):
+            nc.sync.dma_start(c_plane[:].bitcast(I32)[i:P:32, :], c_dealt[:].bitcast(I32)[C_FIRST + i : P : 4, :])
+        k_pool = sbuf("k_pool", [P, POOL], I32, tag="early_then_gate")
+        nc.sync.dma_start(k_pool[:], k_words[0].rearrange("p t r -> p (t r)").bitcast(I32))
 
+        k_dealt = gather("k_dealt", k_bytes[:], U8)
         q_bf = sbuf("q_bf", [P, NQ, PACK], BF16)
         nc.scalar.copy(q_bf[:].rearrange("p (c i) t -> p c t i", i=4), q_raw[:].rearrange("p t (c i) -> p c t i", i=4))
         q_codes = sbuf("q_codes", [P, NQ], U32)
         q_sc = sbuf("q_sc", [P, NQ], U8)
         nc.vector.quantize_mx(out=q_codes[:].bitcast(FP8X4), scales=q_sc[:], in_=q_bf[:].rearrange("p q t -> p (q t)"))
-        place(k_plane, k_dealt, K_FIRST)
+        nc.vector.tensor_copy(k_plane[:].bitcast(I32), k_dealt[:].bitcast(I32))
+        for i in range(1, 4):
+            nc.sync.dma_start(k_plane[:].bitcast(I32)[K_FIRST + i : P : 32, :], k_dealt[:].bitcast(I32)[K_FIRST + ROW_STEP * i : P : 32, :])
 
         c_cols = gather("c_cols", c_pool[:].bitcast(U32), U32)
         k_cols = gather("k_cols", k_pool[:].bitcast(U32), U32)

@@ -46,7 +46,7 @@ def tile_attend_plh_reglu_topk_kernel(tc, qT, k_words, k_scales, c_words, c_scal
         nc.vector.memset(c_plane[:].bitcast(I32), 0)
 
         nc.sync.dma_start(offsets[:], offs)
-        nc.sync.dma_start(c_bytes[:].bitcast(I32)[C_FIRST:, :], c_scales[0].bitcast(I32))
+        nc.scalar.dma_start(c_bytes[:].bitcast(I32)[C_FIRST:, :], c_scales[0].bitcast(I32))
         nc.sync.dma_start(q_raw[:], qT[0].rearrange("(p j) q -> p j q", j=PACK))
         nc.sync.dma_start(k_bytes[:].bitcast(I32)[K_FIRST:P:ROW_STEP, :], k_scales[0].bitcast(I32))
         nc.sync.dma_start(c_pool[:], c_words[0].rearrange("p t r -> p (t r)").bitcast(I32))
@@ -58,13 +58,13 @@ def tile_attend_plh_reglu_topk_kernel(tc, qT, k_words, k_scales, c_words, c_scal
 
         c_dealt = gather("c_dealt", c_bytes[:], U8)
         for i in range(4):
-            nc.sync.dma_start(c_plane[:].bitcast(I32)[i:P:32, :], c_dealt[:].bitcast(I32)[C_FIRST + i : P : 4, :])
+            nc.scalar.dma_start(c_plane[:].bitcast(I32)[i:P:32, :], c_dealt[:].bitcast(I32)[C_FIRST + i : P : 4, :])
         k_pool = sbuf("k_pool", [P, POOL], I32, tag="early_then_gate")
         nc.sync.dma_start(k_pool[:], k_words[0].rearrange("p t r -> p (t r)").bitcast(I32))
 
         k_dealt = gather("k_dealt", k_bytes[:], U8)
         q_bf = sbuf("q_bf", [P, NQ, PACK], BF16)
-        nc.scalar.copy(q_bf[:].rearrange("p (c i) t -> p c t i", i=4), q_raw[:].rearrange("p t (c i) -> p c t i", i=4))
+        nc.vector.tensor_copy(q_bf[:].rearrange("p (c i) t -> p c t i", i=4), q_raw[:].rearrange("p t (c i) -> p c t i", i=4))
         q_codes = sbuf("q_codes", [P, NQ], U32)
         q_sc = sbuf("q_sc", [P, NQ], U8)
         nc.vector.quantize_mx(out=q_codes[:].bitcast(FP8X4), scales=q_sc[:], in_=q_bf[:].rearrange("p q t -> p (q t)"))

@@ -22,6 +22,7 @@ QUARTER = NQ // 4
 K_FIRST = 4
 ROW_STEP = P // ROWS
 C_FIRST = P - ROWS
+K_EARLY = POOL // 2
 
 
 def tile_attend_plh_reglu_topk_kernel(tc, qT, k_words, k_scales, c_words, c_scales, offs, out_0, out_1, out_2):
@@ -30,11 +31,12 @@ def tile_attend_plh_reglu_topk_kernel(tc, qT, k_words, k_scales, c_words, c_scal
         sb = ctx.enter_context(tc.tile_pool(name="sb", bufs=1))
         ps = ctx.enter_context(tc.psum_pool(name="ps", bufs=1))
 
-        def sbuf(name, shape, dtype, tag=""):
-            return sb.tile(shape, dtype, name=name, tag=tag, align_bytes=256)
+        def sbuf(name, shape, dtype):
+            return sb.tile(shape, dtype, name=name, align_bytes=256)
 
         offsets = sb.tile([P, SLOTS // 16], U16, name="offsets")
-        c_bytes = sbuf("c_bytes", [P, POOL], U8, tag="early_then_gate")
+        shared = ctx.enter_context(tc.tile_pool(name="shared", bufs=1))
+        c_bytes = shared.tile([P, POOL], U8, name="c_bytes", align_bytes=256, offset=4 * K_EARLY)
         k_bytes = sbuf("k_bytes", [P, POOL], U8)
         c_pool = sbuf("c_pool", [P, POOL], I32)
         q_raw = sbuf("q_raw", [P, PACK, NQ], F32)
@@ -49,7 +51,9 @@ def tile_attend_plh_reglu_topk_kernel(tc, qT, k_words, k_scales, c_words, c_scal
         nc.scalar.dma_start(c_bytes[:].bitcast(I32)[C_FIRST:, :], c_scales[0].bitcast(I32))
         nc.sync.dma_start(q_raw[:], qT[0].rearrange("(p j) q -> p j q", j=PACK))
         nc.sync.dma_start(k_bytes[:].bitcast(I32)[K_FIRST:P:ROW_STEP, :], k_scales[0].bitcast(I32))
-        nc.sync.dma_start(c_pool[:], c_words[0].rearrange("p t r -> p (t r)").bitcast(I32))
+        c_rows = c_words[0].rearrange("p t r -> p (t r)").bitcast(I32)
+        nc.sync.dma_start(c_pool[:, :K_EARLY], c_rows[:, :K_EARLY])
+        nc.sync.dma_start(c_pool[:, K_EARLY:], c_rows[:, K_EARLY:])
 
         def gather(name, window, dtype):
             dealt = sbuf(name, [P, SLOTS], dtype)
@@ -57,10 +61,12 @@ def tile_attend_plh_reglu_topk_kernel(tc, qT, k_words, k_scales, c_words, c_scal
             return dealt
 
         c_dealt = gather("c_dealt", c_bytes[:], U8)
+        k_pool = shared.tile([P, POOL], I32, name="k_pool", align_bytes=256, offset=0)
+        k_rows = k_words[0].rearrange("p t r -> p (t r)").bitcast(I32)
+        nc.sync.dma_start(k_pool[:, :K_EARLY], k_rows[:, :K_EARLY])
         for i in range(4):
-            nc.scalar.dma_start(c_plane[:].bitcast(I32)[i:P:32, :], c_dealt[:].bitcast(I32)[C_FIRST + i : P : 4, :])
-        k_pool = sbuf("k_pool", [P, POOL], I32, tag="early_then_gate")
-        nc.sync.dma_start(k_pool[:], k_words[0].rearrange("p t r -> p (t r)").bitcast(I32))
+            nc.sync.dma_start(c_plane[:].bitcast(I32)[i:P:32, :], c_dealt[:].bitcast(I32)[C_FIRST + i : P : 4, :])
+        nc.sync.dma_start(k_pool[:, K_EARLY:], k_rows[:, K_EARLY:])
 
         k_dealt = gather("k_dealt", k_bytes[:], U8)
         q_bf = sbuf("q_bf", [P, NQ, PACK], BF16)

@@ -46,6 +46,7 @@ def tile_attend_plh_reglu_topk_kernel(tc, qT, k_words, k_scales, c_words, c_scal
         nc.vector.memset(k_bytes[:].bitcast(I32), 0)
         nc.vector.memset(c_bytes[:].bitcast(I32)[:C_FIRST, :], 0)
         nc.vector.memset(c_plane[:].bitcast(I32), 0)
+        nc.vector.memset(k_plane[:].bitcast(I32), 0)
 
         nc.sync.dma_start(offsets[:], offs)
         nc.scalar.dma_start(c_bytes[:].bitcast(I32)[C_FIRST:, :], c_scales[0].bitcast(I32))
@@ -74,8 +75,7 @@ def tile_attend_plh_reglu_topk_kernel(tc, qT, k_words, k_scales, c_words, c_scal
         q_codes = sbuf("q_codes", [P, NQ], U32)
         q_sc = sbuf("q_sc", [P, NQ], U8)
         nc.vector.quantize_mx(out=q_codes[:].bitcast(FP8X4), scales=q_sc[:], in_=q_bf[:].rearrange("p q t -> p (q t)"))
-        nc.vector.tensor_copy(k_plane[:].bitcast(I32), k_dealt[:].bitcast(I32))
-        for i in range(1, 4):
+        for i in range(4):
             nc.sync.dma_start(k_plane[:].bitcast(I32)[K_FIRST + i : P : 32, :], k_dealt[:].bitcast(I32)[K_FIRST + ROW_STEP * i : P : 32, :])
 
         c_cols = gather("c_cols", c_pool[:].bitcast(U32), U32)
@@ -143,5 +143,5 @@ def tile_attend_plh_reglu_topk_kernel(tc, qT, k_words, k_scales, c_words, c_scal
         quantise(bf_fourth, fourth)
         nc.sync.dma_start(out_words, y_codes[:].bitcast(I32))
         for i in range(4):
-            queue = nc.scalar if i % 2 else nc.sync
+            queue = nc.scalar if i < 2 else nc.sync
             queue.dma_start(out_2[0, i:ROWS:4, :].bitcast(I32), y_sc[i:P:32, :].bitcast(I32))

from contextlib import ExitStack

import concourse.mybir as mybir

SLOTS, POOL, D, NQ = 512, 2048, 512, 256
FLOPS = 2 * 2 * SLOTS * D * NQ

F32 = mybir.dt.float32
BF16 = mybir.dt.bfloat16
I32 = mybir.dt.int32
U32 = mybir.dt.uint32
U16 = mybir.dt.uint16
U8 = mybir.dt.uint8
FP8X4 = mybir.dt.float8_e4m3fn_x4
ALU = mybir.AluOpType

P = 128
PACK = 4
HALF = NQ // 2
ROWS = 16
QUARTER = NQ // 4
K_FIRST = 4
ROW_STEP = P // ROWS
C_FIRST = P - ROWS
K_EARLY = POOL // 2


def tile_attend_plh_reglu_topk_kernel(tc, qT, k_words, k_scales, c_words, c_scales, offs, out_0, out_1, out_2):
    nc = tc.nc
    with ExitStack() as ctx:
        sb = ctx.enter_context(tc.tile_pool(name="sb", bufs=1))
        ps = ctx.enter_context(tc.psum_pool(name="ps", bufs=1))

        def sbuf(name, shape, dtype):
            return sb.tile(shape, dtype, name=name, align_bytes=256)

        offsets = sb.tile([P, SLOTS // 16], U16, name="offsets")
        shared = ctx.enter_context(tc.tile_pool(name="shared", bufs=1))
        c_bytes = shared.tile([P, POOL], U8, name="c_bytes", align_bytes=256, offset=4 * K_EARLY)
        k_bytes = sbuf("k_bytes", [P, POOL], U8)
        c_pool = sbuf("c_pool", [P, POOL], I32)
        q_raw = sbuf("q_raw", [P, PACK, NQ], F32)
        c_plane = sbuf("c_plane", [P, SLOTS], U8)
        k_plane = sbuf("k_plane", [P, SLOTS], U8)

        nc.vector.memset(k_bytes[:].bitcast(I32), 0)
        nc.vector.memset(c_bytes[:].bitcast(I32)[:C_FIRST, :], 0)
        nc.vector.memset(c_plane[:].bitcast(I32), 0)
        nc.vector.memset(k_plane[:].bitcast(I32), 0)

        nc.sync.dma_start(offsets[:], offs)
        nc.scalar.dma_start(c_bytes[:].bitcast(I32)[C_FIRST:, :], c_scales[0].bitcast(I32))
        nc.sync.dma_start(q_raw[:], qT[0].rearrange("(p j) q -> p j q", j=PACK))
        nc.sync.dma_start(k_bytes[:].bitcast(I32)[K_FIRST:P:ROW_STEP, :], k_scales[0].bitcast(I32))
        c_rows = c_words[0].rearrange("p t r -> p (t r)").bitcast(I32)
        nc.sync.dma_start(c_pool[:, :K_EARLY], c_rows[:, :K_EARLY])
        nc.sync.dma_start(c_pool[:, K_EARLY:], c_rows[:, K_EARLY:])

        def gather(name, window, dtype):
            dealt = sbuf(name, [P, SLOTS], dtype)
            nc.vector.tensor_copy(dealt[:].rearrange("p (r s) -> p s r", r=PACK), window.indirect(offsets[:]))
            return dealt

        c_dealt = gather("c_dealt", c_bytes[:], U8)
        k_pool = shared.tile([P, POOL], I32, name="k_pool", align_bytes=256, offset=0)
        k_rows = k_words[0].rearrange("p t r -> p (t r)").bitcast(I32)
        nc.sync.dma_start(k_pool[:, :K_EARLY], k_rows[:, :K_EARLY])
        for i in range(4):
            nc.sync.dma_start(c_plane[:].bitcast(I32)[i:P:32, :], c_dealt[:].bitcast(I32)[C_FIRST + i : P : 4, :])
        nc.sync.dma_start(k_pool[:, K_EARLY:], k_rows[:, K_EARLY:])

        k_dealt = gather("k_dealt", k_bytes[:], U8)
        q_bf = sbuf("q_bf", [P, NQ, PACK], BF16)
        nc.vector.tensor_copy(q_bf[:].rearrange("p (c i) t -> p c t i", i=4), q_raw[:].rearrange("p t (c i) -> p c t i", i=4))
        q_codes = sbuf("q_codes", [P, NQ], U32)
        q_sc = sbuf("q_sc", [P, NQ], U8)
        nc.vector.quantize_mx(out=q_codes[:].bitcast(FP8X4), scales=q_sc[:], in_=q_bf[:].rearrange("p q t -> p (q t)"))
        for i in range(4):
            nc.sync.dma_start(k_plane[:].bitcast(I32)[K_FIRST + i : P : 32, :], k_dealt[:].bitcast(I32)[K_FIRST + ROW_STEP * i : P : 32, :])

        c_cols = gather("c_cols", c_pool[:].bitcast(U32), U32)
        k_cols = gather("k_cols", k_pool[:].bitcast(U32), U32)

        every, low, high = slice(0, NQ), slice(0, HALF), slice(HALF, NQ)
        z_sb = sbuf("z_sb", [P, PACK, NQ], F32)
        y = sbuf("y", [P, PACK, NQ], F32)

        def products(name, bank_no, words, plane, rows, qs):
            bank = ps.tile([P, rows.stop - rows.start, qs.stop - qs.start], F32, name=name, tag=f"bank{bank_no}")
            for r in range(rows.start, rows.stop):
                cols = slice(r * P, (r + 1) * P)
                nc.tensor.matmul_mx(out=bank[:, r - rows.start, :], lhsT=words[:, cols].bitcast(FP8X4), lhsT_scale=plane[:, cols],
                                    rhs=q_codes[:, qs].bitcast(FP8X4), rhs_scale=q_sc[:, qs], start=True, stop=True)
            return bank

        def layer(name, bank_no, rows, qs):
            bank = products(name, bank_no, c_cols, c_plane[:], rows, qs)
            nc.scalar.copy(z_sb[:, rows, qs], bank[:])

        def gate_products(name, bank_no, rows, qs):
            return products(name, bank_no, k_cols, k_plane[K_FIRST:, :], rows, qs)[:], rows, qs

        def gate(piece):
            bank, rows, qs = piece
            nc.vector.scalar_tensor_tensor(out=y[:, rows, qs], in0=bank, scalar=0.0, in1=z_sb[:, rows, qs], op0=ALU.max, op1=ALU.mult)

        out_rows = out_0.rearrange("(p r) q -> p r q", r=PACK)
        out_words = out_1[0].rearrange("p q u -> p (q u)").bitcast(I32)

        third, fourth = slice(HALF, HALF + QUARTER), slice(HALF + QUARTER, NQ)
        for r in range(PACK):
            layer(f"z{r}", r, slice(r, r + 1), every)
        order = [(0, low), (0, high), (1, low), (2, low), (3, low), (1, high), (2, high)]
        for i, (r, qs) in enumerate(order):
            gate(gate_products(f"a{i}", (PACK + i) % 8, slice(r, r + 1), qs))
            if qs == high and r < 2:
                nc.sync.dma_start(out_rows[:, r, :], y[:, r, :])
        last, rows, qs = gate_products("a3_high", PACK - 1, slice(PACK - 1, PACK), high)
        gate((last[:, :, :QUARTER], rows, third))
        gate((last[:, :, QUARTER:], rows, fourth))
        nc.sync.dma_start(out_rows[:, 2:4, :], y[:, 2:4, :])

        y_codes = sbuf("y_codes", [P, NQ], U32)
        y_sc = sbuf("y_sc", [P, NQ], U8)

        def rounded(name, qs, scalar_runs):
            y_bf = sbuf(name, [P, qs.stop - qs.start, PACK], BF16)
            dst = y_bf[:].rearrange("p (c i) t -> p c t i", i=4)
            src = y[:, :, qs].rearrange("p t (c i) -> p c t i", i=4)
            if scalar_runs:
                nc.scalar.copy(dst[:, :scalar_runs], src[:, :scalar_runs])
            nc.vector.tensor_copy(dst[:, scalar_runs:], src[:, scalar_runs:])
            return y_bf

        def quantise(y_bf, qs):
            nc.vector.quantize_mx(out=y_codes[:, qs].bitcast(FP8X4), scales=y_sc[:, qs], in_=y_bf[:].rearrange("p q t -> p (q t)"))

        bf_low = rounded("bf_low", low, 20)
        bf_third = rounded("bf_third", third, 8)
        bf_fourth = rounded("bf_fourth", fourth, 0)
        quantise(bf_low, low)
        quantise(bf_third, third)
        quantise(bf_fourth, fourth)
        nc.sync.dma_start(out_words, y_codes[:].bitcast(I32))
        for i in range(4):
            queue = nc.scalar if i < 2 else nc.sync
            queue.dma_start(out_2[0, i:ROWS:4, :].bitcast(I32), y_sc[i:P:32, :].bitcast(I32))
